import numpy as np
import ml_dtypes


def mxq(x, axis, fmt="e4m3"):
    dtype, down = {"e4m3": (ml_dtypes.float8_e4m3fn, 7), "e5m2": (ml_dtypes.float8_e5m2, 14)}[fmt]
    v = np.moveaxis(np.asarray(x, np.float32).astype(ml_dtypes.bfloat16).astype(np.float64), axis, -1)
    blocks = v.reshape(v.shape[:-1] + (-1, 32))
    amax = np.abs(blocks).max(-1, keepdims=True)
    byte = np.maximum(np.where(amax > 0, np.frexp(amax)[1] - 1 + 127, 0) - down, 1)
    scale = np.exp2(byte - 127.0)
    codes = (blocks / scale).astype(np.float32).astype(dtype).astype(np.float64)
    return np.moveaxis((codes * scale).reshape(v.shape), -1, axis)


WIDE = False


def mx_kscale(k):
    if not WIDE:
        return np.ones(k)
    levels = np.array([10, -10, 5, -5, 0])
    if k % 512:
        return np.exp2(np.random.permutation(np.resize(levels, k // 32))).repeat(32)
    a = np.empty((k // 512, 16))
    for p in range(k // 512):
        a[p, :8] = np.random.permutation(np.resize(levels, 8))
        for g in range(8):
            far = levels[np.abs(levels - a[p, g]) >= 10]
            a[p, g + 8] = far[np.random.randint(len(far))]
    return np.exp2(a.ravel()).repeat(32)


def f64(x):
    return np.asarray(x).astype(np.float64)


def striped(idx):
    return np.tile(np.asarray(idx).reshape(-1, 16).T, (8, 1)).astype(np.uint16)


def unstriped(offs):
    return offs[:16].T.reshape(-1).astype(np.int64)


E2M1 = np.array([0.0, 0.5, 1.0, 1.5, 2.0, 3.0, 4.0, 6.0, -0.0, -0.5, -1.0, -1.5, -2.0, -3.0, -4.0, -6.0])


def pack_weight(w, fmt):
    k, n = w.shape
    w = f64(np.asarray(w, np.float32).astype(ml_dtypes.bfloat16)).reshape(k // 32, 32, n)
    amax = np.abs(w).max(1)
    if fmt == "e4m3":
        byte = np.frexp(amax)[1] - 1 + 127 - 7
    else:
        mant, ex = np.frexp(amax / 6.0)
        byte = np.where(mant > 0.5, ex, ex - 1) + 127
    byte = np.clip(np.where(amax > 0, byte, 1), 1, 254)
    scaled = (w * np.exp2(127.0 - byte)[:, None, :]).reshape(k, n).astype(np.float32)
    by_word = np.ascontiguousarray(scaled.reshape(k // 512, 128, 4, n).transpose(0, 1, 3, 2))
    if fmt == "e4m3":
        words = by_word.astype(ml_dtypes.float8_e4m3fn).view(np.uint8)
    else:
        c = by_word.astype(ml_dtypes.float4_e2m1fn).view(np.uint8) & 0xF
        words = (c[..., 0::2] | (c[..., 1::2] << 4)).reshape(k // 512, 128, 2 * n)
    return np.ascontiguousarray(words), np.ascontiguousarray(byte.astype(np.uint8).reshape(k // 512, 16, n))


def unpack_weight(words, scales, fmt):
    g, _, n = scales.shape
    words = np.ascontiguousarray(words).reshape(g, 128, n, -1)
    if fmt == "e4m3":
        vals = words.view(ml_dtypes.float8_e4m3fn).astype(np.float64)
    else:
        nib = np.empty((g, 128, n, 4), np.uint8)
        nib[..., 0::2] = words & 0xF
        nib[..., 1::2] = words >> 4
        vals = E2M1[nib]
    vals = vals * np.repeat(np.exp2(scales.astype(np.float64) - 127.0), 8, axis=1)[..., None]
    return vals.transpose(0, 1, 3, 2).reshape(g * 512, n)


def bf(x):
    return np.asarray(x, np.float32).astype(ml_dtypes.bfloat16)


def planes(Y):
    r, m = Y.shape
    b = f64(bf(Y)).reshape(r // 32, 32, m)
    amax = np.abs(b).max(1)
    byte = np.clip(np.where(amax > 0, np.frexp(amax)[1] - 1 + 127 - 7, 1), 1, 254)
    codes = (b * np.exp2(127.0 - byte)[:, None, :]).reshape(r, m).astype(np.float32).astype(ml_dtypes.float8_e4m3fn).view(np.uint8)
    words = codes.reshape(r // 512, 128, 4, m).transpose(0, 1, 3, 2)
    return np.ascontiguousarray(words), np.ascontiguousarray(byte.astype(np.uint8).reshape(r // 512, 16, m))


D, C, T, I, Q = 512, 512, 2048, 512, 512


def setup_inputs():
    n = np.random.standard_normal
    idx = np.random.permutation(T)[:I]
    fd = mx_kscale(D)
    fc = mx_kscale(C)
    latp = pack_weight(n((C, T)) / fc[:, None], "e2m1")
    return {
        "query": (n((D, Q)) * 1.0 / np.sqrt(D) * fd[:, None]).astype(np.float32),
        "wuk": (n((D, C)) * 0.8 / np.sqrt(D) / fd[:, None] * fc).astype(np.float32),
        "lat_words": latp[0],
        "lat_scales": latp[1],
        "offs": striped(idx),
    }


def reference(query, wuk, lat_words, lat_scales, offs):
    idx = unstriped(offs)
    latu = unpack_weight(lat_words, lat_scales, "e2m1")
    wukq = mxq(f64(wuk), 0, "e4m3")
    queryq = mxq(f64(query), 0, "e4m3")
    b = wukq.T @ queryq
    bq = mxq(b, 0, "e4m3")
    latidxg = latu[:, idx]
    a = bq.T @ latidxg
    p = np.exp(a - np.max(a, axis=1, keepdims=True))
    y = p / np.sum(p, axis=1, keepdims=True) * 512.0
    words, scales = planes(y)
    return y, words, scales

@@ -1,0 +1,173 @@
+from contextlib import ExitStack
+
+import concourse.mybir as mybir
+
+D, C, T, I, Q = 512, 512, 2048, 512, 512
+FLOPS = 2 * D * C * Q + 2 * C * Q * I
+
+F32 = mybir.dt.float32
+BF16 = mybir.dt.bfloat16
+I32 = mybir.dt.int32
+U32 = mybir.dt.uint32
+U16 = mybir.dt.uint16
+U8 = mybir.dt.uint8
+FP8X4 = mybir.dt.float8_e4m3fn_x4
+FP4X4 = mybir.dt.float4_e2m1fn_x4
+ACT = mybir.ActivationFunctionType
+ALU = mybir.AluOpType
+
+P = 128
+PACK = 4
+OUT_SCALE = 512.0
+Q_HALF = 256
+Q_VECTOR_COLS = 168
+Y_HALF = 256
+Y_VECTOR_COLS = 320
+
+
+def tile_attend_absorbscores_pl_kernel(tc, query, wuk, lat_words, lat_scales, offs, out_0, out_1, out_2):
+    nc = tc.nc
+    with ExitStack() as ctx:
+        sb = ctx.enter_context(tc.tile_pool(name="sb", bufs=1))
+        ps = ctx.enter_context(tc.psum_pool(name="ps", bufs=1))
+
+        offsets = sb.tile([P, I // 16], U16, name="offsets")
+        nc.sync.dma_start(offsets[:], offs)
+
+        lat_sc = sb.tile([P, T], U8, name="lat_sc", tag="lat_sc_then_w_bf", align_bytes=64)
+        nc.vector.memset(lat_sc[:].bitcast(I32), 0)
+        for quad in range(4):
+            nc.scalar.dma_start(
+                lat_sc[32 * quad : 32 * quad + 4, :].bitcast(I32),
+                lat_scales[0, 4 * quad : 4 * quad + 4, :].bitcast(I32),
+            )
+
+        w_raw = sb.tile([P, PACK, C], F32, name="w_raw")
+        nc.sync.dma_start(w_raw[:], wuk.rearrange("(p j) c -> p j c", j=PACK))
+        q_rows = query.rearrange("(p j) q -> p j q", j=PACK)
+        q_raw = []
+        for h in range(Q // Q_HALF):
+            q_half = sb.tile([P, PACK, Q_HALF], F32, name="q_raw%d" % h)
+            nc.sync.dma_start(q_half[:], q_rows[:, :, h * Q_HALF : (h + 1) * Q_HALF])
+            q_raw.append(q_half)
+        lat_w = sb.tile([P, T], U16, name="lat_w", align_bytes=64)
+        nc.sync.dma_start(lat_w[:].bitcast(I32), lat_words[0].bitcast(I32))
+
+        key_sc = sb.tile([P, I], U8, name="key_sc", align_bytes=64)
+        nc.vector.tensor_copy(key_sc[:], lat_sc[:].indirect(offsets[:]))
+
+        w_src = w_raw[:].rearrange("p j (m t) -> p m j t", t=PACK)
+        w_bf_v = sb.tile([P, PACK - 1, P, PACK], BF16, name="w_bf_v", tag="lat_sc_then_w_bf", align_bytes=64)
+        w_bf_s = sb.tile([P, P, PACK], BF16, name="w_bf_s", align_bytes=64)
+        nc.vector.tensor_copy(w_bf_v[:].rearrange("p t m j -> p m j t"), w_src[:, :, :, : PACK - 1])
+        nc.scalar.activation(w_bf_s[:], w_src[:, :, :, PACK - 1], ACT.Copy)
+        w_codes = sb.tile([P, C], U32, name="w_codes", align_bytes=64)
+        w_sc = sb.tile([P, C], U8, name="w_sc", align_bytes=64)
+        for cols, planes in (
+            (slice(0, 2 * P), w_bf_v[:, 0:2].rearrange("p t m j -> p (t m j)")),
+            (slice(2 * P, 3 * P), w_bf_v[:, 2].rearrange("p m j -> p (m j)")),
+            (slice(3 * P, 4 * P), w_bf_s[:].rearrange("p m j -> p (m j)")),
+        ):
+            nc.vector.quantize_mx(w_codes[:, cols].bitcast(FP8X4), w_sc[:, cols], planes)
+
+        b_bf = sb.tile([P, PACK, P, PACK], BF16, name="b_bf", align_bytes=64)
+        for h in range(Q // Q_HALF):
+            q_bf = sb.tile([P, Q_HALF, PACK], BF16, name="q_bf%d" % h, tag="q_bf_then_key_w", align_bytes=64)
+            q_dst = q_bf[:].rearrange("p (g e) j -> p g j e", e=4)
+            q_src = q_raw[h][:].rearrange("p j (g e) -> p g j e", e=4)
+            g_cut = Q_VECTOR_COLS // 4
+            nc.vector.tensor_copy(q_dst[:, :g_cut], q_src[:, :g_cut])
+            nc.scalar.activation(q_dst[:, g_cut:], q_src[:, g_cut:], ACT.Copy)
+            q_codes = sb.tile([P, Q_HALF], U32, name="q_codes%d" % h, align_bytes=64)
+            q_sc = sb.tile([P, Q_HALF], U8, name="q_sc%d" % h, align_bytes=64)
+            nc.vector.quantize_mx(q_codes[:].bitcast(FP8X4), q_sc[:], q_bf[:].rearrange("p q j -> p (q j)"))
+            for v in range(Q_HALF // P):
+                u = h * (Q_HALF // P) + v
+                b_ps = ps.tile([P, PACK, P], F32, name="b_ps%d" % u)
+                for t in range(PACK):
+                    nc.tensor.matmul_mx(
+                        b_ps[:, t, :],
+                        lhsT=w_codes[:, t * P : (t + 1) * P].bitcast(FP8X4),
+                        lhsT_scale=w_sc[:, t * P : (t + 1) * P],
+                        rhs=q_codes[:, v * P : (v + 1) * P].bitcast(FP8X4),
+                        rhs_scale=q_sc[:, v * P : (v + 1) * P],
+                        start=True,
+                        stop=True,
+                    )
+                b_dst = b_bf[:, :, 32 * u : 32 * (u + 1), :]
+                b_src = b_ps[:].rearrange("p t (s r) -> p r s t", r=PACK)
+                if u == 3:
+                    nc.vector.tensor_copy(b_dst, b_src)
+                else:
+                    nc.scalar.activation(b_dst, b_src, ACT.Copy)
+
+        key_w = sb.tile([P, I], U16, name="key_w", tag="q_bf_then_key_w", align_bytes=64)
+        nc.vector.tensor_copy(key_w[:], lat_w[:].indirect(offsets[:]))
+
+        b_codes = sb.tile([P, Q], U32, name="b_codes", align_bytes=64)
+        b_sc = sb.tile([P, Q], U8, name="b_sc", align_bytes=64)
+        neg_max = sb.tile([P, PACK], F32, name="neg_max")
+        row_sum = sb.tile([P, PACK], F32, name="row_sum")
+        inv_sum = sb.tile([P, PACK], F32, name="inv_sum")
+        prob = sb.tile([P, PACK, I], F32, name="prob")
+        y = sb.tile([P, PACK, I], F32, name="y")
+        y_rows = out_0.rearrange("(p r) i -> p r i", r=PACK)
+        a_ps = []
+        for r in range(PACK):
+            cols = slice(r * P, (r + 1) * P)
+            nc.vector.quantize_mx(b_codes[:, cols].bitcast(FP8X4), b_sc[:, cols], b_bf[:, r].rearrange("p s t -> p (s t)"))
+            scores = ps.tile([P, I], F32, name="a_ps%d" % r)
+            nc.tensor.matmul_mx(
+                scores[:],
+                lhsT=b_codes[:, cols].bitcast(FP8X4),
+                lhsT_scale=b_sc[:, cols],
+                rhs=key_w[:].bitcast(FP4X4),
+                rhs_scale=key_sc[:],
+                start=True,
+                stop=True,
+            )
+            a_ps.append(scores)
+
+        def invert(r):
+            nc.vector.reciprocal(inv_sum[:, r : r + 1], row_sum[:, r : r + 1])
+
+        def normalise(r):
+            nc.vector.tensor_scalar(y[:, r, :], prob[:, r, :], inv_sum[:, r : r + 1], OUT_SCALE, ALU.mult, ALU.mult)
+            nc.sync.dma_start(y_rows[:, r, :], y[:, r, :])
+
+        for r in range(PACK):
+            if r == PACK - 1:
+                invert(0)
+            nc.vector.tensor_reduce(neg_max[:, r : r + 1], a_ps[r][:], mybir.AxisListType.X, ALU.max, negate=True)
+            nc.scalar.activation(
+                prob[:, r, :], a_ps[r][:], ACT.Exp, bias=neg_max[:, r : r + 1], scale=1.0, accum_out=row_sum[:, r : r + 1]
+            )
+        invert(1)
+        normalise(0)
+        invert(2)
+        normalise(1)
+        normalise(2)
+        invert(3)
+        normalise(3)
+
+        y_bf = sb.tile([P, I, PACK], BF16, name="y_bf", align_bytes=64)
+        y_dst = y_bf[:].rearrange("p (g e) r -> p g r e", e=4)
+        y_src = y[:].rearrange("p r (g e) -> p g r e", e=4)
+        g_half = Y_HALF // 4
+        g_cut = Y_VECTOR_COLS // 4
+        nc.vector.tensor_copy(y_dst[:, :g_half], y_src[:, :g_half])
+        nc.scalar.activation(y_dst[:, g_cut:], y_src[:, g_cut:], ACT.Copy)
+        nc.vector.tensor_copy(y_dst[:, g_half:g_cut], y_src[:, g_half:g_cut])
+        y_codes = sb.tile([P, I], U32, name="y_codes", align_bytes=64)
+        y_sc = sb.tile([P, I], U8, name="y_sc", align_bytes=64)
+        code_rows = out_1[0].rearrange("p i r -> p (i r)").bitcast(I32)
+        for h in range(I // Y_HALF):
+            cols = slice(h * Y_HALF, (h + 1) * Y_HALF)
+            nc.vector.quantize_mx(y_codes[:, cols].bitcast(FP8X4), y_sc[:, cols], y_bf[:, cols, :].rearrange("p i r -> p (i r)"))
+            nc.sync.dma_start(code_rows[:, cols], y_codes[:, cols].bitcast(I32))
+        for quad in range(4):
+            queue = nc.scalar if quad % 2 == 0 else nc.sync
+            queue.dma_start(
+                out_2[0, 4 * quad : 4 * quad + 4, :].bitcast(I32),
+                y_sc[32 * quad : 32 * quad + 4, :].bitcast(I32),
+            )

@@ -19,8 +19,9 @@ ALU = mybir.AluOpType
 P = 128
 PACK = 4
 OUT_SCALE = 512.0
+W_VECTOR_M = 84
 Q_HALF = 256
-Q_VECTOR_COLS = 168
+Q_VECTOR_COLS = (96, 168)
 Y_HALF = 256
 Y_VECTOR_COLS = 320
 
@@ -34,48 +35,41 @@ def tile_attend_absorbscores_pl_kernel(tc, query, wuk, lat_words, lat_scales, of
         offsets = sb.tile([P, I // 16], U16, name="offsets")
         nc.sync.dma_start(offsets[:], offs)
 
-        lat_sc = sb.tile([P, T], U8, name="lat_sc", tag="lat_sc_then_w_bf", align_bytes=64)
+        lat_sc = sb.tile([P, T], U8, name="lat_sc", align_bytes=64)
         nc.vector.memset(lat_sc[:].bitcast(I32), 0)
-        for quad in range(4):
-            nc.scalar.dma_start(
-                lat_sc[32 * quad : 32 * quad + 4, :].bitcast(I32),
-                lat_scales[0, 4 * quad : 4 * quad + 4, :].bitcast(I32),
-            )
-
         w_raw = sb.tile([P, PACK, C], F32, name="w_raw")
         nc.sync.dma_start(w_raw[:], wuk.rearrange("(p j) c -> p j c", j=PACK))
         q_rows = query.rearrange("(p j) q -> p j q", j=PACK)
         q_raw = []
         for h in range(Q // Q_HALF):
-            q_half = sb.tile([P, PACK, Q_HALF], F32, name="q_raw%d" % h)
+            q_half = sb.tile([P, PACK, Q_HALF], F32, name="q_raw%d" % h, tag="q_raw%d" % h, align_bytes=64)
             nc.sync.dma_start(q_half[:], q_rows[:, :, h * Q_HALF : (h + 1) * Q_HALF])
             q_raw.append(q_half)
+        for quad in range(4):
+            nc.sync.dma_start(
+                lat_sc[32 * quad : 32 * quad + 4, :].bitcast(I32),
+                lat_scales[0, 4 * quad : 4 * quad + 4, :].bitcast(I32),
+            )
+
         lat_w = sb.tile([P, T], U16, name="lat_w", align_bytes=64)
         nc.sync.dma_start(lat_w[:].bitcast(I32), lat_words[0].bitcast(I32))
 
-        key_sc = sb.tile([P, I], U8, name="key_sc", align_bytes=64)
-        nc.vector.tensor_copy(key_sc[:], lat_sc[:].indirect(offsets[:]))
 
+        w_bf = sb.tile([P, PACK, P, PACK], BF16, name="w_bf", align_bytes=64)
+        w_dst = w_bf[:].rearrange("p t m j -> p m j t")
         w_src = w_raw[:].rearrange("p j (m t) -> p m j t", t=PACK)
-        w_bf_v = sb.tile([P, PACK - 1, P, PACK], BF16, name="w_bf_v", tag="lat_sc_then_w_bf", align_bytes=64)
-        w_bf_s = sb.tile([P, P, PACK], BF16, name="w_bf_s", align_bytes=64)
-        nc.vector.tensor_copy(w_bf_v[:].rearrange("p t m j -> p m j t"), w_src[:, :, :, : PACK - 1])
-        nc.scalar.activation(w_bf_s[:], w_src[:, :, :, PACK - 1], ACT.Copy)
+        nc.vector.tensor_copy(w_dst[:, :W_VECTOR_M], w_src[:, :W_VECTOR_M])
+        nc.scalar.activation(w_dst[:, W_VECTOR_M:], w_src[:, W_VECTOR_M:], ACT.Copy)
         w_codes = sb.tile([P, C], U32, name="w_codes", align_bytes=64)
         w_sc = sb.tile([P, C], U8, name="w_sc", align_bytes=64)
-        for cols, planes in (
-            (slice(0, 2 * P), w_bf_v[:, 0:2].rearrange("p t m j -> p (t m j)")),
-            (slice(2 * P, 3 * P), w_bf_v[:, 2].rearrange("p m j -> p (m j)")),
-            (slice(3 * P, 4 * P), w_bf_s[:].rearrange("p m j -> p (m j)")),
-        ):
-            nc.vector.quantize_mx(w_codes[:, cols].bitcast(FP8X4), w_sc[:, cols], planes)
+        nc.vector.quantize_mx(w_codes[:].bitcast(FP8X4), w_sc[:], w_bf[:].rearrange("p t m j -> p (t m j)"))
 
         b_bf = sb.tile([P, PACK, P, PACK], BF16, name="b_bf", align_bytes=64)
         for h in range(Q // Q_HALF):
-            q_bf = sb.tile([P, Q_HALF, PACK], BF16, name="q_bf%d" % h, tag="q_bf_then_key_w", align_bytes=64)
+            q_bf = sb.tile([P, Q_HALF, PACK], BF16, name="q_bf%d" % h, tag="q_bf", align_bytes=64)
             q_dst = q_bf[:].rearrange("p (g e) j -> p g j e", e=4)
             q_src = q_raw[h][:].rearrange("p j (g e) -> p g j e", e=4)
-            g_cut = Q_VECTOR_COLS // 4
+            g_cut = Q_VECTOR_COLS[h] // 4
             nc.vector.tensor_copy(q_dst[:, :g_cut], q_src[:, :g_cut])
             nc.scalar.activation(q_dst[:, g_cut:], q_src[:, g_cut:], ACT.Copy)
             q_codes = sb.tile([P, Q_HALF], U32, name="q_codes%d" % h, align_bytes=64)
@@ -96,12 +90,11 @@ def tile_attend_absorbscores_pl_kernel(tc, query, wuk, lat_words, lat_scales, of
                     )
                 b_dst = b_bf[:, :, 32 * u : 32 * (u + 1), :]
                 b_src = b_ps[:].rearrange("p t (s r) -> p r s t", r=PACK)
-                if u == 3:
-                    nc.vector.tensor_copy(b_dst, b_src)
-                else:
-                    nc.scalar.activation(b_dst, b_src, ACT.Copy)
+                nc.scalar.activation(b_dst, b_src, ACT.Copy)
 
-        key_w = sb.tile([P, I], U16, name="key_w", tag="q_bf_then_key_w", align_bytes=64)
+        key_sc = sb.tile([P, I], U8, name="key_sc", tag="q_bf", align_bytes=64)
+        nc.vector.tensor_copy(key_sc[:], lat_sc[:].indirect(offsets[:]))
+        key_w = sb.tile([P, I], U16, name="key_w", tag="q_raw1", align_bytes=64)
         nc.vector.tensor_copy(key_w[:], lat_w[:].indirect(offsets[:]))
 
         b_codes = sb.tile([P, Q], U32, name="b_codes", align_bytes=64)
@@ -132,7 +125,10 @@ def tile_attend_absorbscores_pl_kernel(tc, query, wuk, lat_words, lat_scales, of
             nc.vector.reciprocal(inv_sum[:, r : r + 1], row_sum[:, r : r + 1])
 
         def normalise(r):
-            nc.vector.tensor_scalar(y[:, r, :], prob[:, r, :], inv_sum[:, r : r + 1], OUT_SCALE, ALU.mult, ALU.mult)
+            width = Y_HALF if r == PACK - 1 else I
+            for first in range(0, I, width):
+                cols = slice(first, first + width)
+                nc.vector.tensor_scalar(y[:, r, cols], prob[:, r, cols], inv_sum[:, r : r + 1], OUT_SCALE, ALU.mult, ALU.mult)
             nc.sync.dma_start(y_rows[:, r, :], y[:, r, :])
 
         for r in range(PACK):

@@ -21,9 +21,9 @@ PACK = 4
 OUT_SCALE = 512.0
 W_VECTOR_M = 84
 Q_HALF = 256
-Q_VECTOR_COLS = (96, 168)
+Q_VECTOR_COLS = 168
 Y_HALF = 256
-Y_VECTOR_COLS = 320
+Y_VECTOR_COLS = 304
 
 
 def tile_attend_absorbscores_pl_kernel(tc, query, wuk, lat_words, lat_scales, offs, out_0, out_1, out_2):
@@ -36,8 +36,15 @@ def tile_attend_absorbscores_pl_kernel(tc, query, wuk, lat_words, lat_scales, of
         nc.sync.dma_start(offsets[:], offs)
 
         lat_sc = sb.tile([P, T], U8, name="lat_sc", align_bytes=64)
-        nc.vector.memset(lat_sc[:].bitcast(I32), 0)
-        w_raw = sb.tile([P, PACK, C], F32, name="w_raw")
+        nc.sync.dma_start(lat_sc[16:32, :].bitcast(I32), lat_scales[0].bitcast(I32))
+        nc.vector.memset(lat_sc[0:16, :].bitcast(I32), 0)
+        nc.gpsimd.memset(lat_sc[32:64, :].bitcast(I32), 0)
+        nc.vector.memset(lat_sc[64:P, :].bitcast(I32), 0)
+        key_sc = sb.tile([P, I], U8, name="key_sc", align_bytes=64)
+        nc.vector.memset(key_sc[:].bitcast(I32), 0)
+        listed_sc = sb.tile([P, I], U8, name="listed_sc", align_bytes=64)
+        nc.vector.tensor_copy(listed_sc[:], lat_sc[:].indirect(offsets[:]))
+        w_raw = sb.tile([P, PACK, C], F32, name="w_raw", tag="w_raw", align_bytes=64)
         nc.sync.dma_start(w_raw[:], wuk.rearrange("(p j) c -> p j c", j=PACK))
         q_rows = query.rearrange("(p j) q -> p j q", j=PACK)
         q_raw = []
@@ -45,15 +52,14 @@ def tile_attend_absorbscores_pl_kernel(tc, query, wuk, lat_words, lat_scales, of
             q_half = sb.tile([P, PACK, Q_HALF], F32, name="q_raw%d" % h, tag="q_raw%d" % h, align_bytes=64)
             nc.sync.dma_start(q_half[:], q_rows[:, :, h * Q_HALF : (h + 1) * Q_HALF])
             q_raw.append(q_half)
+
+        lat_w = sb.tile([P, T], U16, name="lat_w", tag="lat_w", align_bytes=64)
+        nc.sync.dma_start(lat_w[:].bitcast(I32), lat_words[0].bitcast(I32))
         for quad in range(4):
             nc.sync.dma_start(
-                lat_sc[32 * quad : 32 * quad + 4, :].bitcast(I32),
-                lat_scales[0, 4 * quad : 4 * quad + 4, :].bitcast(I32),
+                key_sc[32 * quad : 32 * quad + 4, :].bitcast(I32),
+                listed_sc[16 + 4 * quad : 20 + 4 * quad, :].bitcast(I32),
             )
-
-        lat_w = sb.tile([P, T], U16, name="lat_w", align_bytes=64)
-        nc.sync.dma_start(lat_w[:].bitcast(I32), lat_words[0].bitcast(I32))
-
 
         w_bf = sb.tile([P, PACK, P, PACK], BF16, name="w_bf", align_bytes=64)
         w_dst = w_bf[:].rearrange("p t m j -> p m j t")
@@ -66,17 +72,26 @@ def tile_attend_absorbscores_pl_kernel(tc, query, wuk, lat_words, lat_scales, of
 
         b_bf = sb.tile([P, PACK, P, PACK], BF16, name="b_bf", align_bytes=64)
         for h in range(Q // Q_HALF):
-            q_bf = sb.tile([P, Q_HALF, PACK], BF16, name="q_bf%d" % h, tag="q_bf", align_bytes=64)
+            q_bf = sb.tile([P, Q_HALF, PACK], BF16, name="q_bf%d" % h, tag=("q_bf0", "q_raw0")[h], align_bytes=64)
             q_dst = q_bf[:].rearrange("p (g e) j -> p g j e", e=4)
             q_src = q_raw[h][:].rearrange("p j (g e) -> p g j e", e=4)
-            g_cut = Q_VECTOR_COLS[h] // 4
-            nc.vector.tensor_copy(q_dst[:, :g_cut], q_src[:, :g_cut])
-            nc.scalar.activation(q_dst[:, g_cut:], q_src[:, g_cut:], ACT.Copy)
+            g_bank = P // 4
+            if h == 0:
+                nc.scalar.activation(q_dst[:, :g_bank], q_src[:, :g_bank], ACT.Copy)
+                nc.scalar.activation(q_dst[:, g_bank:], q_src[:, g_bank:], ACT.Copy)
+            else:
+                g_cut = Q_VECTOR_COLS // 4
+                nc.vector.tensor_copy(q_dst[:, :g_bank], q_src[:, :g_bank])
+                nc.scalar.activation(q_dst[:, g_cut:], q_src[:, g_cut:], ACT.Copy)
+                nc.vector.tensor_copy(q_dst[:, g_bank:g_cut], q_src[:, g_bank:g_cut])
             q_codes = sb.tile([P, Q_HALF], U32, name="q_codes%d" % h, align_bytes=64)
             q_sc = sb.tile([P, Q_HALF], U8, name="q_sc%d" % h, align_bytes=64)
-            nc.vector.quantize_mx(q_codes[:].bitcast(FP8X4), q_sc[:], q_bf[:].rearrange("p q j -> p (q j)"))
             for v in range(Q_HALF // P):
                 u = h * (Q_HALF // P) + v
+                bank_cols = slice(v * P, (v + 1) * P)
+                nc.vector.quantize_mx(
+                    q_codes[:, bank_cols].bitcast(FP8X4), q_sc[:, bank_cols], q_bf[:, bank_cols, :].rearrange("p q j -> p (q j)")
+                )
                 b_ps = ps.tile([P, PACK, P], F32, name="b_ps%d" % u)
                 for t in range(PACK):
                     nc.tensor.matmul_mx(
@@ -92,12 +107,10 @@ def tile_attend_absorbscores_pl_kernel(tc, query, wuk, lat_words, lat_scales, of
                 b_src = b_ps[:].rearrange("p t (s r) -> p r s t", r=PACK)
                 nc.scalar.activation(b_dst, b_src, ACT.Copy)
 
-        key_sc = sb.tile([P, I], U8, name="key_sc", tag="q_bf", align_bytes=64)
-        nc.vector.tensor_copy(key_sc[:], lat_sc[:].indirect(offsets[:]))
         key_w = sb.tile([P, I], U16, name="key_w", tag="q_raw1", align_bytes=64)
         nc.vector.tensor_copy(key_w[:], lat_w[:].indirect(offsets[:]))
 
-        b_codes = sb.tile([P, Q], U32, name="b_codes", align_bytes=64)
+        b_codes = sb.tile([P, Q], U32, name="b_codes", tag="lat_w", align_bytes=64)
         b_sc = sb.tile([P, Q], U8, name="b_sc", align_bytes=64)
         neg_max = sb.tile([P, PACK], F32, name="neg_max")
         row_sum = sb.tile([P, PACK], F32, name="row_sum")
@@ -124,13 +137,13 @@ def tile_attend_absorbscores_pl_kernel(tc, query, wuk, lat_words, lat_scales, of
         def invert(r):
             nc.vector.reciprocal(inv_sum[:, r : r + 1], row_sum[:, r : r + 1])
 
-        def normalise(r):
-            width = Y_HALF if r == PACK - 1 else I
-            for first in range(0, I, width):
-                cols = slice(first, first + width)
-                nc.vector.tensor_scalar(y[:, r, cols], prob[:, r, cols], inv_sum[:, r : r + 1], OUT_SCALE, ALU.mult, ALU.mult)
+        def normalise(r, cols):
+            nc.vector.tensor_scalar(y[:, r, cols], prob[:, r, cols], inv_sum[:, r : r + 1], OUT_SCALE, ALU.mult, ALU.mult)
+
+        def store(r):
             nc.sync.dma_start(y_rows[:, r, :], y[:, r, :])
 
+        low, high, whole = slice(0, Y_HALF), slice(Y_HALF, I), slice(0, I)
         for r in range(PACK):
             if r == PACK - 1:
                 invert(0)
@@ -139,12 +152,20 @@ def tile_attend_absorbscores_pl_kernel(tc, query, wuk, lat_words, lat_scales, of
                 prob[:, r, :], a_ps[r][:], ACT.Exp, bias=neg_max[:, r : r + 1], scale=1.0, accum_out=row_sum[:, r : r + 1]
             )
         invert(1)
-        normalise(0)
+        factor = sb.tile([P, 1], F32, name="factor")
+        nc.vector.tensor_scalar(factor[:], inv_sum[:, 0:1], OUT_SCALE, None, ALU.mult)
+        nc.scalar.activation(y[:, 0, :], prob[:, 0, :], ACT.Copy, scale=factor[:])
         invert(2)
-        normalise(1)
-        normalise(2)
+        normalise(1, whole)
+        store(1)
+        normalise(2, low)
         invert(3)
-        normalise(3)
+        normalise(2, high)
+        store(2)
+        store(0)
+        normalise(3, high)
+        normalise(3, low)
+        store(3)
 
         y_bf = sb.tile([P, I, PACK], BF16, name="y_bf", align_bytes=64)
         y_dst = y_bf[:].rearrange("p (g e) r -> p g r e", e=4)

@@ -19,9 +19,9 @@ ALU = mybir.AluOpType
 P = 128
 PACK = 4
 OUT_SCALE = 512.0
+SCALE_ROW = P - 16
 W_VECTOR_M = 84
 Q_HALF = 256
-Q_VECTOR_COLS = 168
 Y_HALF = 256
 Y_VECTOR_COLS = 304
 
@@ -36,10 +36,8 @@ def tile_attend_absorbscores_pl_kernel(tc, query, wuk, lat_words, lat_scales, of
         nc.sync.dma_start(offsets[:], offs)
 
         lat_sc = sb.tile([P, T], U8, name="lat_sc", align_bytes=64)
-        nc.sync.dma_start(lat_sc[16:32, :].bitcast(I32), lat_scales[0].bitcast(I32))
-        nc.vector.memset(lat_sc[0:16, :].bitcast(I32), 0)
-        nc.gpsimd.memset(lat_sc[32:64, :].bitcast(I32), 0)
-        nc.vector.memset(lat_sc[64:P, :].bitcast(I32), 0)
+        nc.sync.dma_start(lat_sc[SCALE_ROW:, :].bitcast(I32), lat_scales[0].bitcast(I32))
+        nc.vector.memset(lat_sc[:SCALE_ROW, :].bitcast(I32), 0)
         key_sc = sb.tile([P, I], U8, name="key_sc", align_bytes=64)
         nc.vector.memset(key_sc[:].bitcast(I32), 0)
         listed_sc = sb.tile([P, I], U8, name="listed_sc", align_bytes=64)
@@ -58,7 +56,7 @@ def tile_attend_absorbscores_pl_kernel(tc, query, wuk, lat_words, lat_scales, of
         for quad in range(4):
             nc.sync.dma_start(
                 key_sc[32 * quad : 32 * quad + 4, :].bitcast(I32),
-                listed_sc[16 + 4 * quad : 20 + 4 * quad, :].bitcast(I32),
+                listed_sc[SCALE_ROW + 4 * quad : SCALE_ROW + 4 * quad + 4, :].bitcast(I32),
             )
 
         w_bf = sb.tile([P, PACK, P, PACK], BF16, name="w_bf", align_bytes=64)
@@ -72,25 +70,21 @@ def tile_attend_absorbscores_pl_kernel(tc, query, wuk, lat_words, lat_scales, of
 
         b_bf = sb.tile([P, PACK, P, PACK], BF16, name="b_bf", align_bytes=64)
         for h in range(Q // Q_HALF):
-            q_bf = sb.tile([P, Q_HALF, PACK], BF16, name="q_bf%d" % h, tag=("q_bf0", "q_raw0")[h], align_bytes=64)
-            q_dst = q_bf[:].rearrange("p (g e) j -> p g j e", e=4)
-            q_src = q_raw[h][:].rearrange("p j (g e) -> p g j e", e=4)
-            g_bank = P // 4
+            q_bf = sb.tile([P, PACK, Q_HALF // PACK, PACK], BF16, name="q_bf%d" % h, tag=("q_bf0", "q_raw0")[h], align_bytes=64)
+            q_dst = q_bf[:].rearrange("p r s j -> p s j r")
+            q_src = q_raw[h][:].rearrange("p j (s r) -> p s j r", r=PACK)
+            nc.scalar.activation(q_dst[:, :, :, :2], q_src[:, :, :, :2], ACT.Copy)
             if h == 0:
-                nc.scalar.activation(q_dst[:, :g_bank], q_src[:, :g_bank], ACT.Copy)
-                nc.scalar.activation(q_dst[:, g_bank:], q_src[:, g_bank:], ACT.Copy)
+                nc.scalar.activation(q_dst[:, :, :, 2:], q_src[:, :, :, 2:], ACT.Copy)
             else:
-                g_cut = Q_VECTOR_COLS // 4
-                nc.vector.tensor_copy(q_dst[:, :g_bank], q_src[:, :g_bank])
-                nc.scalar.activation(q_dst[:, g_cut:], q_src[:, g_cut:], ACT.Copy)
-                nc.vector.tensor_copy(q_dst[:, g_bank:g_cut], q_src[:, g_bank:g_cut])
+                nc.vector.tensor_copy(q_dst[:, :, :, 2:], q_src[:, :, :, 2:])
             q_codes = sb.tile([P, Q_HALF], U32, name="q_codes%d" % h, align_bytes=64)
             q_sc = sb.tile([P, Q_HALF], U8, name="q_sc%d" % h, align_bytes=64)
             for v in range(Q_HALF // P):
                 u = h * (Q_HALF // P) + v
                 bank_cols = slice(v * P, (v + 1) * P)
                 nc.vector.quantize_mx(
-                    q_codes[:, bank_cols].bitcast(FP8X4), q_sc[:, bank_cols], q_bf[:, bank_cols, :].rearrange("p q j -> p (q j)")
+                    q_codes[:, bank_cols].bitcast(FP8X4), q_sc[:, bank_cols], q_bf[:, 2 * v : 2 * v + 2].rearrange("p r s j -> p (r s j)")
                 )
                 b_ps = ps.tile([P, PACK, P], F32, name="b_ps%d" % u)
                 for t in range(PACK):
@@ -103,8 +97,8 @@ def tile_attend_absorbscores_pl_kernel(tc, query, wuk, lat_words, lat_scales, of
                         start=True,
                         stop=True,
                     )
-                b_dst = b_bf[:, :, 32 * u : 32 * (u + 1), :]
-                b_src = b_ps[:].rearrange("p t (s r) -> p r s t", r=PACK)
+                b_dst = b_bf[:, 2 * v : 2 * v + 2, 64 * h : 64 * (h + 1), :]
+                b_src = b_ps[:].rearrange("p t (r s) -> p r s t", r=2)
                 nc.scalar.activation(b_dst, b_src, ACT.Copy)
 
         key_w = sb.tile([P, I], U16, name="key_w", tag="q_raw1", align_bytes=64)

@@ -18,12 +18,15 @@ ALU = mybir.AluOpType
 
 P = 128
 PACK = 4
+QUADS = 4
 OUT_SCALE = 512.0
-SCALE_ROW = P - 16
+FIRST_SCALE_ROW = P - 16
+Q_HALF = Q // 2
+S_HALF = Q_HALF // PACK
+Y_HALF = I // 2
+RUN = 4
 W_VECTOR_M = 84
-Q_HALF = 256
-Y_HALF = 256
-Y_VECTOR_COLS = 304
+Y_VECTOR_COLS = 320
 
 
 def tile_attend_absorbscores_pl_kernel(tc, query, wuk, lat_words, lat_scales, offs, out_0, out_1, out_2):
@@ -36,12 +39,13 @@ def tile_attend_absorbscores_pl_kernel(tc, query, wuk, lat_words, lat_scales, of
         nc.sync.dma_start(offsets[:], offs)
 
         lat_sc = sb.tile([P, T], U8, name="lat_sc", align_bytes=64)
-        nc.sync.dma_start(lat_sc[SCALE_ROW:, :].bitcast(I32), lat_scales[0].bitcast(I32))
-        nc.vector.memset(lat_sc[:SCALE_ROW, :].bitcast(I32), 0)
+        nc.sync.dma_start(lat_sc[FIRST_SCALE_ROW:, :].bitcast(I32), lat_scales[0].bitcast(I32))
+        nc.vector.memset(lat_sc[:FIRST_SCALE_ROW, :].bitcast(I32), 0)
         key_sc = sb.tile([P, I], U8, name="key_sc", align_bytes=64)
         nc.vector.memset(key_sc[:].bitcast(I32), 0)
         listed_sc = sb.tile([P, I], U8, name="listed_sc", align_bytes=64)
         nc.vector.tensor_copy(listed_sc[:], lat_sc[:].indirect(offsets[:]))
+
         w_raw = sb.tile([P, PACK, C], F32, name="w_raw", tag="w_raw", align_bytes=64)
         nc.sync.dma_start(w_raw[:], wuk.rearrange("(p j) c -> p j c", j=PACK))
         q_rows = query.rearrange("(p j) q -> p j q", j=PACK)
@@ -50,13 +54,13 @@ def tile_attend_absorbscores_pl_kernel(tc, query, wuk, lat_words, lat_scales, of
             q_half = sb.tile([P, PACK, Q_HALF], F32, name="q_raw%d" % h, tag="q_raw%d" % h, align_bytes=64)
             nc.sync.dma_start(q_half[:], q_rows[:, :, h * Q_HALF : (h + 1) * Q_HALF])
             q_raw.append(q_half)
-
         lat_w = sb.tile([P, T], U16, name="lat_w", tag="lat_w", align_bytes=64)
         nc.sync.dma_start(lat_w[:].bitcast(I32), lat_words[0].bitcast(I32))
-        for quad in range(4):
+
+        for quad in range(QUADS):
             nc.sync.dma_start(
                 key_sc[32 * quad : 32 * quad + 4, :].bitcast(I32),
-                listed_sc[SCALE_ROW + 4 * quad : SCALE_ROW + 4 * quad + 4, :].bitcast(I32),
+                listed_sc[FIRST_SCALE_ROW + 4 * quad : FIRST_SCALE_ROW + 4 * quad + 4, :].bitcast(I32),
             )
 
         w_bf = sb.tile([P, PACK, P, PACK], BF16, name="w_bf", align_bytes=64)
@@ -70,7 +74,7 @@ def tile_attend_absorbscores_pl_kernel(tc, query, wuk, lat_words, lat_scales, of
 
         b_bf = sb.tile([P, PACK, P, PACK], BF16, name="b_bf", align_bytes=64)
         for h in range(Q // Q_HALF):
-            q_bf = sb.tile([P, PACK, Q_HALF // PACK, PACK], BF16, name="q_bf%d" % h, tag=("q_bf0", "q_raw0")[h], align_bytes=64)
+            q_bf = sb.tile([P, PACK, S_HALF, PACK], BF16, name="q_bf%d" % h, tag=("q_bf0", "q_raw0")[h], align_bytes=64)
             q_dst = q_bf[:].rearrange("p r s j -> p s j r")
             q_src = q_raw[h][:].rearrange("p j (s r) -> p s j r", r=PACK)
             nc.scalar.activation(q_dst[:, :, :, :2], q_src[:, :, :, :2], ACT.Copy)
@@ -80,26 +84,26 @@ def tile_attend_absorbscores_pl_kernel(tc, query, wuk, lat_words, lat_scales, of
                 nc.vector.tensor_copy(q_dst[:, :, :, 2:], q_src[:, :, :, 2:])
             q_codes = sb.tile([P, Q_HALF], U32, name="q_codes%d" % h, align_bytes=64)
             q_sc = sb.tile([P, Q_HALF], U8, name="q_sc%d" % h, align_bytes=64)
-            for v in range(Q_HALF // P):
-                u = h * (Q_HALF // P) + v
-                bank_cols = slice(v * P, (v + 1) * P)
+            for v in range(2):
+                pair_cols = slice(v * P, (v + 1) * P)
                 nc.vector.quantize_mx(
-                    q_codes[:, bank_cols].bitcast(FP8X4), q_sc[:, bank_cols], q_bf[:, 2 * v : 2 * v + 2].rearrange("p r s j -> p (r s j)")
+                    q_codes[:, pair_cols].bitcast(FP8X4),
+                    q_sc[:, pair_cols],
+                    q_bf[:, 2 * v : 2 * v + 2].rearrange("p r s j -> p (r s j)"),
                 )
-                b_ps = ps.tile([P, PACK, P], F32, name="b_ps%d" % u)
+                b_ps = ps.tile([P, PACK, P], F32, name="b_ps%d" % (2 * h + v))
                 for t in range(PACK):
                     nc.tensor.matmul_mx(
                         b_ps[:, t, :],
                         lhsT=w_codes[:, t * P : (t + 1) * P].bitcast(FP8X4),
                         lhsT_scale=w_sc[:, t * P : (t + 1) * P],
-                        rhs=q_codes[:, v * P : (v + 1) * P].bitcast(FP8X4),
-                        rhs_scale=q_sc[:, v * P : (v + 1) * P],
+                        rhs=q_codes[:, pair_cols].bitcast(FP8X4),
+                        rhs_scale=q_sc[:, pair_cols],
                         start=True,
                         stop=True,
                     )
-                b_dst = b_bf[:, 2 * v : 2 * v + 2, 64 * h : 64 * (h + 1), :]
-                b_src = b_ps[:].rearrange("p t (r s) -> p r s t", r=2)
-                nc.scalar.activation(b_dst, b_src, ACT.Copy)
+                b_dst = b_bf[:, 2 * v : 2 * v + 2, S_HALF * h : S_HALF * (h + 1), :]
+                nc.scalar.activation(b_dst, b_ps[:].rearrange("p t (r s) -> p r s t", r=2), ACT.Copy)
 
         key_w = sb.tile([P, I], U16, name="key_w", tag="q_raw1", align_bytes=64)
         nc.vector.tensor_copy(key_w[:], lat_w[:].indirect(offsets[:]))
@@ -112,71 +116,80 @@ def tile_attend_absorbscores_pl_kernel(tc, query, wuk, lat_words, lat_scales, of
         prob = sb.tile([P, PACK, I], F32, name="prob")
         y = sb.tile([P, PACK, I], F32, name="y")
         y_rows = out_0.rearrange("(p r) i -> p r i", r=PACK)
+
         a_ps = []
-        for r in range(PACK):
-            cols = slice(r * P, (r + 1) * P)
-            nc.vector.quantize_mx(b_codes[:, cols].bitcast(FP8X4), b_sc[:, cols], b_bf[:, r].rearrange("p s t -> p (s t)"))
-            scores = ps.tile([P, I], F32, name="a_ps%d" % r)
-            nc.tensor.matmul_mx(
-                scores[:],
-                lhsT=b_codes[:, cols].bitcast(FP8X4),
-                lhsT_scale=b_sc[:, cols],
-                rhs=key_w[:].bitcast(FP4X4),
-                rhs_scale=key_sc[:],
-                start=True,
-                stop=True,
+        for first, last in ((0, 1), (1, 2), (2, PACK)):
+            made = slice(first * P, last * P)
+            nc.vector.quantize_mx(
+                b_codes[:, made].bitcast(FP8X4), b_sc[:, made], b_bf[:, first:last].rearrange("p r s t -> p (r s t)")
             )
-            a_ps.append(scores)
+            for r in range(first, last):
+                tile_cols = slice(r * P, (r + 1) * P)
+                scores = ps.tile([P, I], F32, name="a_ps%d" % r)
+                nc.tensor.matmul_mx(
+                    scores[:],
+                    lhsT=b_codes[:, tile_cols].bitcast(FP8X4),
+                    lhsT_scale=b_sc[:, tile_cols],
+                    rhs=key_w[:].bitcast(FP4X4),
+                    rhs_scale=key_sc[:],
+                    start=True,
+                    stop=True,
+                )
+                a_ps.append(scores)
 
-        def invert(r):
-            nc.vector.reciprocal(inv_sum[:, r : r + 1], row_sum[:, r : r + 1])
+        def exponentiate(r):
+            nc.vector.tensor_reduce(neg_max[:, r : r + 1], a_ps[r][:], mybir.AxisListType.X, ALU.max, negate=True)
+            nc.scalar.activation(
+                prob[:, r, :], a_ps[r][:], ACT.Exp, bias=neg_max[:, r : r + 1], scale=1.0, accum_out=row_sum[:, r : r + 1]
+            )
 
-        def normalise(r, cols):
-            nc.vector.tensor_scalar(y[:, r, cols], prob[:, r, cols], inv_sum[:, r : r + 1], OUT_SCALE, ALU.mult, ALU.mult)
+        def invert(first, last):
+            nc.vector.reciprocal(inv_sum[:, first:last], row_sum[:, first:last])
+
+        def normalise(r, slots):
+            nc.vector.tensor_scalar(y[:, r, slots], prob[:, r, slots], inv_sum[:, r : r + 1], OUT_SCALE, ALU.mult, ALU.mult)
 
         def store(r):
             nc.sync.dma_start(y_rows[:, r, :], y[:, r, :])
 
         low, high, whole = slice(0, Y_HALF), slice(Y_HALF, I), slice(0, I)
-        for r in range(PACK):
-            if r == PACK - 1:
-                invert(0)
-            nc.vector.tensor_reduce(neg_max[:, r : r + 1], a_ps[r][:], mybir.AxisListType.X, ALU.max, negate=True)
-            nc.scalar.activation(
-                prob[:, r, :], a_ps[r][:], ACT.Exp, bias=neg_max[:, r : r + 1], scale=1.0, accum_out=row_sum[:, r : r + 1]
-            )
-        invert(1)
+        for r in range(PACK - 1):
+            exponentiate(r)
+        invert(0, 2)
+        exponentiate(3)
         factor = sb.tile([P, 1], F32, name="factor")
         nc.vector.tensor_scalar(factor[:], inv_sum[:, 0:1], OUT_SCALE, None, ALU.mult)
         nc.scalar.activation(y[:, 0, :], prob[:, 0, :], ACT.Copy, scale=factor[:])
-        invert(2)
+        invert(2, 3)
         normalise(1, whole)
         store(1)
         normalise(2, low)
-        invert(3)
+        invert(3, 4)
         normalise(2, high)
         store(2)
         store(0)
-        normalise(3, high)
         normalise(3, low)
+        normalise(3, high)
         store(3)
 
         y_bf = sb.tile([P, I, PACK], BF16, name="y_bf", align_bytes=64)
-        y_dst = y_bf[:].rearrange("p (g e) r -> p g r e", e=4)
-        y_src = y[:].rearrange("p r (g e) -> p g r e", e=4)
-        g_half = Y_HALF // 4
-        g_cut = Y_VECTOR_COLS // 4
+        y_dst = y_bf[:].rearrange("p (g e) r -> p g r e", e=RUN)
+        y_src = y[:].rearrange("p r (g e) -> p g r e", e=RUN)
+        g_half = Y_HALF // RUN
+        g_cut = Y_VECTOR_COLS // RUN
         nc.vector.tensor_copy(y_dst[:, :g_half], y_src[:, :g_half])
         nc.scalar.activation(y_dst[:, g_cut:], y_src[:, g_cut:], ACT.Copy)
         nc.vector.tensor_copy(y_dst[:, g_half:g_cut], y_src[:, g_half:g_cut])
         y_codes = sb.tile([P, I], U32, name="y_codes", align_bytes=64)
         y_sc = sb.tile([P, I], U8, name="y_sc", align_bytes=64)
         code_rows = out_1[0].rearrange("p i r -> p (i r)").bitcast(I32)
-        for h in range(I // Y_HALF):
-            cols = slice(h * Y_HALF, (h + 1) * Y_HALF)
-            nc.vector.quantize_mx(y_codes[:, cols].bitcast(FP8X4), y_sc[:, cols], y_bf[:, cols, :].rearrange("p i r -> p (i r)"))
-            nc.sync.dma_start(code_rows[:, cols], y_codes[:, cols].bitcast(I32))
-        for quad in range(4):
+        for first in range(0, I, Y_HALF):
+            slots = slice(first, first + Y_HALF)
+            nc.vector.quantize_mx(
+                y_codes[:, slots].bitcast(FP8X4), y_sc[:, slots], y_bf[:, slots, :].rearrange("p i r -> p (i r)")
+            )
+            nc.sync.dma_start(code_rows[:, slots], y_codes[:, slots].bitcast(I32))
+        for quad in range(QUADS):
             queue = nc.scalar if quad % 2 == 0 else nc.sync
             queue.dma_start(
                 out_2[0, 4 * quad : 4 * quad + 4, :].bitcast(I32),

@@ -26,6 +26,7 @@ S_HALF = Q_HALF // PACK
 Y_HALF = I // 2
 RUN = 4
 W_VECTOR_M = 84
+Q_VECTOR_S = 20
 Y_VECTOR_COLS = 320
 
 
@@ -77,10 +78,12 @@ def tile_attend_absorbscores_pl_kernel(tc, query, wuk, lat_words, lat_scales, of
             q_bf = sb.tile([P, PACK, S_HALF, PACK], BF16, name="q_bf%d" % h, tag=("q_bf0", "q_raw0")[h], align_bytes=64)
             q_dst = q_bf[:].rearrange("p r s j -> p s j r")
             q_src = q_raw[h][:].rearrange("p j (s r) -> p s j r", r=PACK)
-            nc.scalar.activation(q_dst[:, :, :, :2], q_src[:, :, :, :2], ACT.Copy)
             if h == 0:
+                nc.scalar.activation(q_dst[:, :, :, :2], q_src[:, :, :, :2], ACT.Copy)
                 nc.scalar.activation(q_dst[:, :, :, 2:], q_src[:, :, :, 2:], ACT.Copy)
             else:
+                nc.scalar.activation(q_dst[:, Q_VECTOR_S:, :, :2], q_src[:, Q_VECTOR_S:, :, :2], ACT.Copy)
+                nc.vector.tensor_copy(q_dst[:, :Q_VECTOR_S, :, :2], q_src[:, :Q_VECTOR_S, :, :2])
                 nc.vector.tensor_copy(q_dst[:, :, :, 2:], q_src[:, :, :, 2:])
             q_codes = sb.tile([P, Q_HALF], U32, name="q_codes%d" % h, align_bytes=64)
             q_sc = sb.tile([P, Q_HALF], U8, name="q_sc%d" % h, align_bytes=64)
@@ -143,8 +146,8 @@ def tile_attend_absorbscores_pl_kernel(tc, query, wuk, lat_words, lat_scales, of
                 prob[:, r, :], a_ps[r][:], ACT.Exp, bias=neg_max[:, r : r + 1], scale=1.0, accum_out=row_sum[:, r : r + 1]
             )
 
-        def invert(first, last):
-            nc.vector.reciprocal(inv_sum[:, first:last], row_sum[:, first:last])
+        def invert(r):
+            nc.vector.reciprocal(inv_sum[:, r : r + 1], row_sum[:, r : r + 1])
 
         def normalise(r, slots):
             nc.vector.tensor_scalar(y[:, r, slots], prob[:, r, slots], inv_sum[:, r : r + 1], OUT_SCALE, ALU.mult, ALU.mult)
@@ -155,19 +158,20 @@ def tile_attend_absorbscores_pl_kernel(tc, query, wuk, lat_words, lat_scales, of
         low, high, whole = slice(0, Y_HALF), slice(Y_HALF, I), slice(0, I)
         for r in range(PACK - 1):
             exponentiate(r)
-        invert(0, 2)
+        invert(0)
         exponentiate(3)
+        normalise(0, whole)
+        store(0)
+        invert(1)
+        invert(2)
         factor = sb.tile([P, 1], F32, name="factor")
-        nc.vector.tensor_scalar(factor[:], inv_sum[:, 0:1], OUT_SCALE, None, ALU.mult)
-        nc.scalar.activation(y[:, 0, :], prob[:, 0, :], ACT.Copy, scale=factor[:])
-        invert(2, 3)
-        normalise(1, whole)
-        store(1)
+        nc.vector.tensor_scalar(factor[:], inv_sum[:, 1:2], OUT_SCALE, None, ALU.mult)
+        nc.scalar.activation(y[:, 1, :], prob[:, 1, :], ACT.Copy, scale=factor[:])
         normalise(2, low)
-        invert(3, 4)
+        invert(3)
         normalise(2, high)
         store(2)
-        store(0)
+        store(1)
         normalise(3, low)
         normalise(3, high)
         store(3)

@@ -25,8 +25,8 @@ Q_HALF = Q // 2
 S_HALF = Q_HALF // PACK
 Y_HALF = I // 2
 RUN = 4
-W_VECTOR_M = 84
-Q_VECTOR_S = 20
+W_VECTOR_M = 88
+Q_VECTOR_S = 32
 Y_VECTOR_COLS = 320
 
 

@@ -25,7 +25,7 @@ Q_HALF = Q // 2
 S_HALF = Q_HALF // PACK
 Y_HALF = I // 2
 RUN = 4
-W_VECTOR_M = 88
+W_VECTOR_M = 44
 Q_VECTOR_S = 32
 Y_VECTOR_COLS = 320
 
@@ -47,11 +47,14 @@ def tile_attend_absorbscores_pl_kernel(tc, query, wuk, lat_words, lat_scales, of
         listed_sc = sb.tile([P, I], U8, name="listed_sc", align_bytes=64)
         nc.vector.tensor_copy(listed_sc[:], lat_sc[:].indirect(offsets[:]))
 
-        w_raw = sb.tile([P, PACK, C], F32, name="w_raw", tag="w_raw", align_bytes=64)
-        nc.sync.dma_start(w_raw[:], wuk.rearrange("(p j) c -> p j c", j=PACK))
+        w_rows = wuk.rearrange("(p j) c -> p j c", j=PACK)
         q_rows = query.rearrange("(p j) q -> p j q", j=PACK)
+        w_raw = []
         q_raw = []
-        for h in range(Q // Q_HALF):
+        for h in range(2):
+            w_half = sb.tile([P, PACK, C // 2], F32, name="w_raw%d" % h, tag="w_raw%d" % h, align_bytes=64)
+            nc.sync.dma_start(w_half[:], w_rows[:, :, h * (C // 2) : (h + 1) * (C // 2)])
+            w_raw.append(w_half)
             q_half = sb.tile([P, PACK, Q_HALF], F32, name="q_raw%d" % h, tag="q_raw%d" % h, align_bytes=64)
             nc.sync.dma_start(q_half[:], q_rows[:, :, h * Q_HALF : (h + 1) * Q_HALF])
             q_raw.append(q_half)
@@ -64,49 +67,67 @@ def tile_attend_absorbscores_pl_kernel(tc, query, wuk, lat_words, lat_scales, of
                 listed_sc[FIRST_SCALE_ROW + 4 * quad : FIRST_SCALE_ROW + 4 * quad + 4, :].bitcast(I32),
             )
 
-        w_bf = sb.tile([P, PACK, P, PACK], BF16, name="w_bf", align_bytes=64)
-        w_dst = w_bf[:].rearrange("p t m j -> p m j t")
-        w_src = w_raw[:].rearrange("p j (m t) -> p m j t", t=PACK)
-        nc.vector.tensor_copy(w_dst[:, :W_VECTOR_M], w_src[:, :W_VECTOR_M])
-        nc.scalar.activation(w_dst[:, W_VECTOR_M:], w_src[:, W_VECTOR_M:], ACT.Copy)
         w_codes = sb.tile([P, C], U32, name="w_codes", align_bytes=64)
         w_sc = sb.tile([P, C], U8, name="w_sc", align_bytes=64)
-        nc.vector.quantize_mx(w_codes[:].bitcast(FP8X4), w_sc[:], w_bf[:].rearrange("p t m j -> p (t m j)"))
-
         b_bf = sb.tile([P, PACK, P, PACK], BF16, name="b_bf", align_bytes=64)
-        for h in range(Q // Q_HALF):
-            q_bf = sb.tile([P, PACK, S_HALF, PACK], BF16, name="q_bf%d" % h, tag=("q_bf0", "q_raw0")[h], align_bytes=64)
-            q_dst = q_bf[:].rearrange("p r s j -> p s j r")
-            q_src = q_raw[h][:].rearrange("p j (s r) -> p s j r", r=PACK)
-            if h == 0:
-                nc.scalar.activation(q_dst[:, :, :, :2], q_src[:, :, :, :2], ACT.Copy)
-                nc.scalar.activation(q_dst[:, :, :, 2:], q_src[:, :, :, 2:], ACT.Copy)
-            else:
-                nc.scalar.activation(q_dst[:, Q_VECTOR_S:, :, :2], q_src[:, Q_VECTOR_S:, :, :2], ACT.Copy)
-                nc.vector.tensor_copy(q_dst[:, :Q_VECTOR_S, :, :2], q_src[:, :Q_VECTOR_S, :, :2])
-                nc.vector.tensor_copy(q_dst[:, :, :, 2:], q_src[:, :, :, 2:])
-            q_codes = sb.tile([P, Q_HALF], U32, name="q_codes%d" % h, align_bytes=64)
-            q_sc = sb.tile([P, Q_HALF], U8, name="q_sc%d" % h, align_bytes=64)
-            for v in range(2):
-                pair_cols = slice(v * P, (v + 1) * P)
+        M_HALF = P // 2
+
+        def round_pairs(name, raw, shares):
+            src = raw[:].rearrange("p j (m t) -> p m j t", t=PACK)
+            pairs = []
+            for u in range(2):
+                pair = sb.tile([P, 2, M_HALF, PACK], BF16, name="%s%d" % (name, u), tag="pair%d" % u, align_bytes=64)
+                dst = pair[:].rearrange("p t m j -> p m j t")
+                cut = shares[u]
+                nc.vector.tensor_copy(dst[:, :cut], src[:, :cut, :, 2 * u : 2 * u + 2])
+                if cut < M_HALF:
+                    nc.scalar.activation(dst[:, cut:], src[:, cut:, :, 2 * u : 2 * u + 2], ACT.Copy)
+                pairs.append(pair)
+            return pairs
+
+        def quantise_w(h, pairs):
+            for t in range(PACK):
+                cols = slice(t * P + h * M_HALF, t * P + (h + 1) * M_HALF)
                 nc.vector.quantize_mx(
-                    q_codes[:, pair_cols].bitcast(FP8X4),
-                    q_sc[:, pair_cols],
-                    q_bf[:, 2 * v : 2 * v + 2].rearrange("p r s j -> p (r s j)"),
+                    w_codes[:, cols].bitcast(FP8X4), w_sc[:, cols], pairs[t // 2][:, t % 2].rearrange("p m j -> p (m j)")
                 )
-                b_ps = ps.tile([P, PACK, P], F32, name="b_ps%d" % (2 * h + v))
-                for t in range(PACK):
-                    nc.tensor.matmul_mx(
-                        b_ps[:, t, :],
-                        lhsT=w_codes[:, t * P : (t + 1) * P].bitcast(FP8X4),
-                        lhsT_scale=w_sc[:, t * P : (t + 1) * P],
-                        rhs=q_codes[:, pair_cols].bitcast(FP8X4),
-                        rhs_scale=q_sc[:, pair_cols],
-                        start=True,
-                        stop=True,
-                    )
-                b_dst = b_bf[:, 2 * v : 2 * v + 2, S_HALF * h : S_HALF * (h + 1), :]
-                nc.scalar.activation(b_dst, b_ps[:].rearrange("p t (r s) -> p r s t", r=2), ACT.Copy)
+
+        def quantise_q(h, v, pair):
+            pair_cols = slice(v * P, (v + 1) * P)
+            nc.vector.quantize_mx(
+                q_codes[h][:, pair_cols].bitcast(FP8X4), q_sc[h][:, pair_cols], pair[:].rearrange("p r s j -> p (r s j)")
+            )
+
+        q_codes = [sb.tile([P, Q_HALF], U32, name="q_codes%d" % h, align_bytes=64) for h in range(2)]
+        q_sc = [sb.tile([P, Q_HALF], U8, name="q_sc%d" % h, align_bytes=64) for h in range(2)]
+
+        def bank(h, v):
+            pair_cols = slice(v * P, (v + 1) * P)
+            b_ps = ps.tile([P, PACK, P], F32, name="b_ps%d" % (2 * h + v))
+            for t in range(PACK):
+                nc.tensor.matmul_mx(
+                    b_ps[:, t, :],
+                    lhsT=w_codes[:, t * P : (t + 1) * P].bitcast(FP8X4),
+                    lhsT_scale=w_sc[:, t * P : (t + 1) * P],
+                    rhs=q_codes[h][:, pair_cols].bitcast(FP8X4),
+                    rhs_scale=q_sc[h][:, pair_cols],
+                    start=True,
+                    stop=True,
+                )
+            b_dst = b_bf[:, 2 * v : 2 * v + 2, S_HALF * h : S_HALF * (h + 1), :]
+            nc.scalar.activation(b_dst, b_ps[:].rearrange("p t (r s) -> p r s t", r=2), ACT.Copy)
+
+        quantise_w(0, round_pairs("w_lo", w_raw[0], (44, 44)))
+        pairs = round_pairs("q_lo", q_raw[0], (44, 44))
+        for v in range(2):
+            quantise_q(0, v, pairs[v])
+        quantise_w(1, round_pairs("w_hi", w_raw[1], (40, 44)))
+        bank(0, 0)
+        bank(0, 1)
+        pairs = round_pairs("q_hi", q_raw[1], (Q_VECTOR_S, M_HALF))
+        for v in range(2):
+            quantise_q(1, v, pairs[v])
+            bank(1, v)
 
         key_w = sb.tile([P, I], U16, name="key_w", tag="q_raw1", align_bytes=64)
         nc.vector.tensor_copy(key_w[:], lat_w[:].indirect(offsets[:]))

@@ -20,12 +20,10 @@ P = 128
 PACK = 4
 QUADS = 4
 OUT_SCALE = 512.0
-FIRST_SCALE_ROW = P - 16
 Q_HALF = Q // 2
 S_HALF = Q_HALF // PACK
 Y_HALF = I // 2
 RUN = 4
-W_VECTOR_M = 44
 Q_VECTOR_S = 32
 Y_VECTOR_COLS = 320
 
@@ -36,54 +34,48 @@ def tile_attend_absorbscores_pl_kernel(tc, query, wuk, lat_words, lat_scales, of
         sb = ctx.enter_context(tc.tile_pool(name="sb", bufs=1))
         ps = ctx.enter_context(tc.psum_pool(name="ps", bufs=1))
 
-        offsets = sb.tile([P, I // 16], U16, name="offsets")
-        nc.sync.dma_start(offsets[:], offs)
-
-        lat_sc = sb.tile([P, T], U8, name="lat_sc", align_bytes=64)
-        nc.sync.dma_start(lat_sc[FIRST_SCALE_ROW:, :].bitcast(I32), lat_scales[0].bitcast(I32))
-        nc.vector.memset(lat_sc[:FIRST_SCALE_ROW, :].bitcast(I32), 0)
-        key_sc = sb.tile([P, I], U8, name="key_sc", align_bytes=64)
-        nc.vector.memset(key_sc[:].bitcast(I32), 0)
-        listed_sc = sb.tile([P, I], U8, name="listed_sc", align_bytes=64)
-        nc.vector.tensor_copy(listed_sc[:], lat_sc[:].indirect(offsets[:]))
-
         w_rows = wuk.rearrange("(p j) c -> p j c", j=PACK)
         q_rows = query.rearrange("(p j) q -> p j q", j=PACK)
-        w_raw = []
-        q_raw = []
-        for h in range(2):
-            w_half = sb.tile([P, PACK, C // 2], F32, name="w_raw%d" % h, tag="w_raw%d" % h, align_bytes=64)
-            nc.sync.dma_start(w_half[:], w_rows[:, :, h * (C // 2) : (h + 1) * (C // 2)])
-            w_raw.append(w_half)
-            q_half = sb.tile([P, PACK, Q_HALF], F32, name="q_raw%d" % h, tag="q_raw%d" % h, align_bytes=64)
-            nc.sync.dma_start(q_half[:], q_rows[:, :, h * Q_HALF : (h + 1) * Q_HALF])
-            q_raw.append(q_half)
+
+        def load_half(name, rows, h):
+            half = sb.tile([P, PACK, Q_HALF], F32, name="%s%d" % (name, h), tag="%s%d" % (name, h), align_bytes=64)
+            nc.sync.dma_start(half[:], rows[:, :, h * Q_HALF : (h + 1) * Q_HALF])
+            return half
+
+        lat_sc = sb.tile([P, T], U8, name="lat_sc", align_bytes=64)
+        nc.vector.memset(lat_sc[:].bitcast(I32), 0)
+        w_raw = [load_half("w_raw", w_rows, 0)]
+        offsets = sb.tile([P, I // 16], U16, name="offsets")
+        nc.sync.dma_start(offsets[:], offs)
+        nc.sync.dma_start(lat_sc[32:96:4, :].bitcast(I32), lat_scales[0].bitcast(I32))
+        key_sc = sb.tile([P, I], U8, name="key_sc", align_bytes=64)
+        nc.vector.memset(key_sc[:].bitcast(I32), 0)
+        q_raw = [load_half("q_raw", q_rows, 0)]
+        w_raw.append(load_half("w_raw", w_rows, 1))
+        q_raw.append(load_half("q_raw", q_rows, 1))
         lat_w = sb.tile([P, T], U16, name="lat_w", tag="lat_w", align_bytes=64)
         nc.sync.dma_start(lat_w[:].bitcast(I32), lat_words[0].bitcast(I32))
-
-        for quad in range(QUADS):
-            nc.sync.dma_start(
-                key_sc[32 * quad : 32 * quad + 4, :].bitcast(I32),
-                listed_sc[FIRST_SCALE_ROW + 4 * quad : FIRST_SCALE_ROW + 4 * quad + 4, :].bitcast(I32),
-            )
 
         w_codes = sb.tile([P, C], U32, name="w_codes", align_bytes=64)
         w_sc = sb.tile([P, C], U8, name="w_sc", align_bytes=64)
         b_bf = sb.tile([P, PACK, P, PACK], BF16, name="b_bf", align_bytes=64)
         M_HALF = P // 2
 
-        def round_pairs(name, raw, shares):
+        def pair_tiles(name, tag, places):
+            return [
+                sb.tile([P, 2, places, PACK], BF16, name="%s%d" % (name, u), tag="%s%d" % (tag, u), align_bytes=64)
+                for u in range(2)
+            ]
+
+        def round_pairs(pairs, first, raw, shares):
             src = raw[:].rearrange("p j (m t) -> p m j t", t=PACK)
-            pairs = []
             for u in range(2):
-                pair = sb.tile([P, 2, M_HALF, PACK], BF16, name="%s%d" % (name, u), tag="pair%d" % u, align_bytes=64)
-                dst = pair[:].rearrange("p t m j -> p m j t")
+                dst = pairs[u][:, :, first : first + M_HALF, :].rearrange("p t m j -> p m j t")
                 cut = shares[u]
-                nc.vector.tensor_copy(dst[:, :cut], src[:, :cut, :, 2 * u : 2 * u + 2])
+                if cut > 0:
+                    nc.vector.tensor_copy(dst[:, :cut], src[:, :cut, :, 2 * u : 2 * u + 2])
                 if cut < M_HALF:
                     nc.scalar.activation(dst[:, cut:], src[:, cut:, :, 2 * u : 2 * u + 2], ACT.Copy)
-                pairs.append(pair)
-            return pairs
 
         def quantise_w(h, pairs):
             for t in range(PACK):
@@ -117,14 +109,28 @@ def tile_attend_absorbscores_pl_kernel(tc, query, wuk, lat_words, lat_scales, of
             b_dst = b_bf[:, 2 * v : 2 * v + 2, S_HALF * h : S_HALF * (h + 1), :]
             nc.scalar.activation(b_dst, b_ps[:].rearrange("p t (r s) -> p r s t", r=2), ACT.Copy)
 
-        quantise_w(0, round_pairs("w_lo", w_raw[0], (44, 44)))
-        pairs = round_pairs("q_lo", q_raw[0], (44, 44))
+        pairs = pair_tiles("w_lo", "w_pair", M_HALF)
+        round_pairs(pairs, 0, w_raw[0], (0, 0))
+        listed_sc = sb.tile([P, I], U8, name="listed_sc", align_bytes=64)
+        nc.vector.tensor_copy(listed_sc[:], lat_sc[:].indirect(offsets[:]))
+        for quad in range(QUADS):
+            nc.sync.dma_start(
+                key_sc[32 * quad : 32 * quad + 4, :].bitcast(I32),
+                listed_sc[32 + 16 * quad : 48 + 16 * quad : 4, :].bitcast(I32),
+            )
+
+        quantise_w(0, pairs)
+        pairs = pair_tiles("q_lo", "pair", M_HALF)
+        round_pairs(pairs, 0, q_raw[0], (0, 16))
         for v in range(2):
             quantise_q(0, v, pairs[v])
-        quantise_w(1, round_pairs("w_hi", w_raw[1], (40, 44)))
+        pairs = pair_tiles("w_hi", "pair", M_HALF)
+        round_pairs(pairs, 0, w_raw[1], (28, 44))
+        quantise_w(1, pairs)
         bank(0, 0)
         bank(0, 1)
-        pairs = round_pairs("q_hi", q_raw[1], (Q_VECTOR_S, M_HALF))
+        pairs = pair_tiles("q_hi", "pair", M_HALF)
+        round_pairs(pairs, 0, q_raw[1], (Q_VECTOR_S, M_HALF))
         for v in range(2):
             quantise_q(1, v, pairs[v])
             bank(1, v)

@@ -61,11 +61,8 @@ def tile_attend_absorbscores_pl_kernel(tc, query, wuk, lat_words, lat_scales, of
         b_bf = sb.tile([P, PACK, P, PACK], BF16, name="b_bf", align_bytes=64)
         M_HALF = P // 2
 
-        def pair_tiles(name, tag, places):
-            return [
-                sb.tile([P, 2, places, PACK], BF16, name="%s%d" % (name, u), tag="%s%d" % (tag, u), align_bytes=64)
-                for u in range(2)
-            ]
+        def pair_tiles(name, tags):
+            return [sb.tile([P, 2, M_HALF, PACK], BF16, name="%s%d" % (name, u), tag=tags[u], align_bytes=64) for u in range(2)]
 
         def round_pairs(pairs, first, raw, shares):
             src = raw[:].rearrange("p j (m t) -> p m j t", t=PACK)
@@ -84,33 +81,29 @@ def tile_attend_absorbscores_pl_kernel(tc, query, wuk, lat_words, lat_scales, of
                     w_codes[:, cols].bitcast(FP8X4), w_sc[:, cols], pairs[t // 2][:, t % 2].rearrange("p m j -> p (m j)")
                 )
 
-        def quantise_q(h, v, pair):
-            pair_cols = slice(v * P, (v + 1) * P)
-            nc.vector.quantize_mx(
-                q_codes[h][:, pair_cols].bitcast(FP8X4), q_sc[h][:, pair_cols], pair[:].rearrange("p r s j -> p (r s j)")
-            )
+        def quantise_q(name, pair, tag):
+            codes = sb.tile([P, P], U32, name=name + "_codes", tag=tag, align_bytes=64)
+            scales = sb.tile([P, P], U8, name=name + "_sc", align_bytes=64)
+            nc.vector.quantize_mx(codes[:].bitcast(FP8X4), scales[:], pair[:].rearrange("p r s j -> p (r s j)"))
+            return codes, scales
 
-        q_codes = [sb.tile([P, Q_HALF], U32, name="q_codes%d" % h, align_bytes=64) for h in range(2)]
-        q_sc = [sb.tile([P, Q_HALF], U8, name="q_sc%d" % h, align_bytes=64) for h in range(2)]
-
-        def bank(h, v):
-            pair_cols = slice(v * P, (v + 1) * P)
+        def bank(h, v, operand):
             b_ps = ps.tile([P, PACK, P], F32, name="b_ps%d" % (2 * h + v))
             for t in range(PACK):
                 nc.tensor.matmul_mx(
                     b_ps[:, t, :],
                     lhsT=w_codes[:, t * P : (t + 1) * P].bitcast(FP8X4),
                     lhsT_scale=w_sc[:, t * P : (t + 1) * P],
-                    rhs=q_codes[h][:, pair_cols].bitcast(FP8X4),
-                    rhs_scale=q_sc[h][:, pair_cols],
+                    rhs=operand[0][:].bitcast(FP8X4),
+                    rhs_scale=operand[1][:],
                     start=True,
                     stop=True,
                 )
             b_dst = b_bf[:, 2 * v : 2 * v + 2, S_HALF * h : S_HALF * (h + 1), :]
             nc.scalar.activation(b_dst, b_ps[:].rearrange("p t (r s) -> p r s t", r=2), ACT.Copy)
 
-        pairs = pair_tiles("w_lo", "w_pair", M_HALF)
-        round_pairs(pairs, 0, w_raw[0], (0, 0))
+        w_lo = pair_tiles("w_lo", ("buf_a", "buf_b"))
+        round_pairs(w_lo, 0, w_raw[0], (0, 0))
         listed_sc = sb.tile([P, I], U8, name="listed_sc", align_bytes=64)
         nc.vector.tensor_copy(listed_sc[:], lat_sc[:].indirect(offsets[:]))
         for quad in range(QUADS):
@@ -119,21 +112,19 @@ def tile_attend_absorbscores_pl_kernel(tc, query, wuk, lat_words, lat_scales, of
                 listed_sc[32 + 16 * quad : 48 + 16 * quad : 4, :].bitcast(I32),
             )
 
-        quantise_w(0, pairs)
-        pairs = pair_tiles("q_lo", "pair", M_HALF)
-        round_pairs(pairs, 0, q_raw[0], (0, 16))
+        quantise_w(0, w_lo)
+        q_lo = pair_tiles("q_lo", ("buf_c", "buf_d"))
+        round_pairs(q_lo, 0, q_raw[0], (0, 16))
+        first = quantise_q("q00", q_lo[0], "q00_codes")
+        w_hi = pair_tiles("w_hi", ("buf_c", "buf_b"))
+        round_pairs(w_hi, 0, w_raw[1], (36, 44))
+        quantise_w(1, w_hi)
+        bank(0, 0, first)
+        bank(0, 1, quantise_q("q01", q_lo[1], "buf_c"))
+        q_hi = pair_tiles("q_hi", ("buf_b", "buf_d"))
+        round_pairs(q_hi, 0, q_raw[1], (Q_VECTOR_S, M_HALF))
         for v in range(2):
-            quantise_q(0, v, pairs[v])
-        pairs = pair_tiles("w_hi", "pair", M_HALF)
-        round_pairs(pairs, 0, w_raw[1], (28, 44))
-        quantise_w(1, pairs)
-        bank(0, 0)
-        bank(0, 1)
-        pairs = pair_tiles("q_hi", "pair", M_HALF)
-        round_pairs(pairs, 0, q_raw[1], (Q_VECTOR_S, M_HALF))
-        for v in range(2):
-            quantise_q(1, v, pairs[v])
-            bank(1, v)
+            bank(1, v, quantise_q("q1%d" % v, q_hi[v], "q1%d_codes" % v))
 
         key_w = sb.tile([P, I], U16, name="key_w", tag="q_raw1", align_bytes=64)
         nc.vector.tensor_copy(key_w[:], lat_w[:].indirect(offsets[:]))

@@ -212,7 +212,7 @@ def tile_attend_absorbscores_pl_kernel(tc, query, wuk, lat_words, lat_scales, of
             )
             nc.sync.dma_start(code_rows[:, slots], y_codes[:, slots].bitcast(I32))
         for quad in range(QUADS):
-            queue = nc.scalar if quad % 2 == 0 else nc.sync
+            queue = nc.scalar if quad == 0 else nc.sync
             queue.dma_start(
                 out_2[0, 4 * quad : 4 * quad + 4, :].bitcast(I32),
                 y_sc[32 * quad : 32 * quad + 4, :].bitcast(I32),

@@ -50,6 +50,13 @@ def tile_attend_absorbscores_pl_kernel(tc, query, wuk, lat_words, lat_scales, of
         nc.sync.dma_start(lat_sc[32:96:4, :].bitcast(I32), lat_scales[0].bitcast(I32))
         key_sc = sb.tile([P, I], U8, name="key_sc", align_bytes=64)
         nc.vector.memset(key_sc[:].bitcast(I32), 0)
+        zeros = sb.tile([P, P], BF16, name="zeros", align_bytes=64)
+        zero_codes = sb.tile([P, I], U32, name="zero_codes", align_bytes=64)
+        zero_sc = sb.tile([P, P], U8, name="zero_sc", align_bytes=64)
+        nc.vector.memset(zeros[:].bitcast(I32), 0)
+        nc.vector.memset(zero_codes[:].bitcast(I32), 0)
+        nc.vector.memset(zero_sc[:].bitcast(I32), 0)
+        nc.vector.quantize_mx(zero_codes[:, : P // PACK].bitcast(FP8X4), zero_sc[:, : P // PACK], zeros[:])
         q_raw = [load_half("q_raw", q_rows, 0)]
         w_raw.append(load_half("w_raw", w_rows, 1))
         q_raw.append(load_half("q_raw", q_rows, 1))
@@ -106,6 +113,17 @@ def tile_attend_absorbscores_pl_kernel(tc, query, wuk, lat_words, lat_scales, of
         round_pairs(w_lo, 0, w_raw[0], (0, 0))
         listed_sc = sb.tile([P, I], U8, name="listed_sc", align_bytes=64)
         nc.vector.tensor_copy(listed_sc[:], lat_sc[:].indirect(offsets[:]))
+        warm_ps = ps.tile([P, I], F32, name="warm_ps", tag="a_ps3")
+        for warm in range(2):
+            nc.tensor.matmul_mx(
+                warm_ps[:],
+                lhsT=zero_codes[:, :P].bitcast(FP8X4),
+                lhsT_scale=zero_sc[:],
+                rhs=zero_codes[:].bitcast(FP8X4),
+                rhs_scale=listed_sc[:],
+                start=True,
+                stop=True,
+            )
         for quad in range(QUADS):
             nc.sync.dma_start(
                 key_sc[32 * quad : 32 * quad + 4, :].bitcast(I32),
@@ -146,7 +164,7 @@ def tile_attend_absorbscores_pl_kernel(tc, query, wuk, lat_words, lat_scales, of
             )
             for r in range(first, last):
                 tile_cols = slice(r * P, (r + 1) * P)
-                scores = ps.tile([P, I], F32, name="a_ps%d" % r)
+                scores = ps.tile([P, I], F32, name="a_ps%d" % r, tag="a_ps%d" % r)
                 nc.tensor.matmul_mx(
                     scores[:],
                     lhsT=b_codes[:, tile_cols].bitcast(FP8X4),

@@ -50,13 +50,6 @@ def tile_attend_absorbscores_pl_kernel(tc, query, wuk, lat_words, lat_scales, of
         nc.sync.dma_start(lat_sc[32:96:4, :].bitcast(I32), lat_scales[0].bitcast(I32))
         key_sc = sb.tile([P, I], U8, name="key_sc", align_bytes=64)
         nc.vector.memset(key_sc[:].bitcast(I32), 0)
-        zeros = sb.tile([P, P], BF16, name="zeros", align_bytes=64)
-        zero_codes = sb.tile([P, I], U32, name="zero_codes", align_bytes=64)
-        zero_sc = sb.tile([P, P], U8, name="zero_sc", align_bytes=64)
-        nc.vector.memset(zeros[:].bitcast(I32), 0)
-        nc.vector.memset(zero_codes[:].bitcast(I32), 0)
-        nc.vector.memset(zero_sc[:].bitcast(I32), 0)
-        nc.vector.quantize_mx(zero_codes[:, : P // PACK].bitcast(FP8X4), zero_sc[:, : P // PACK], zeros[:])
         q_raw = [load_half("q_raw", q_rows, 0)]
         w_raw.append(load_half("w_raw", w_rows, 1))
         q_raw.append(load_half("q_raw", q_rows, 1))
@@ -113,17 +106,6 @@ def tile_attend_absorbscores_pl_kernel(tc, query, wuk, lat_words, lat_scales, of
         round_pairs(w_lo, 0, w_raw[0], (0, 0))
         listed_sc = sb.tile([P, I], U8, name="listed_sc", align_bytes=64)
         nc.vector.tensor_copy(listed_sc[:], lat_sc[:].indirect(offsets[:]))
-        warm_ps = ps.tile([P, I], F32, name="warm_ps", tag="a_ps3")
-        for warm in range(2):
-            nc.tensor.matmul_mx(
-                warm_ps[:],
-                lhsT=zero_codes[:, :P].bitcast(FP8X4),
-                lhsT_scale=zero_sc[:],
-                rhs=zero_codes[:].bitcast(FP8X4),
-                rhs_scale=listed_sc[:],
-                start=True,
-                stop=True,
-            )
         for quad in range(QUADS):
             nc.sync.dma_start(
                 key_sc[32 * quad : 32 * quad + 4, :].bitcast(I32),
@@ -134,6 +116,17 @@ def tile_attend_absorbscores_pl_kernel(tc, query, wuk, lat_words, lat_scales, of
         q_lo = pair_tiles("q_lo", ("buf_c", "buf_d"))
         round_pairs(q_lo, 0, q_raw[0], (0, 16))
         first = quantise_q("q00", q_lo[0], "q00_codes")
+        warm_ps = ps.tile([32, P], F32, name="warm_ps", tag="a_ps3")
+        for warm in range(6):
+            nc.tensor.matmul_mx(
+                warm_ps[:],
+                lhsT=first[0][:, :32].bitcast(FP8X4),
+                lhsT_scale=first[1][:, :32],
+                rhs=first[0][:].bitcast(FP8X4),
+                rhs_scale=first[1][:],
+                start=True,
+                stop=True,
+            )
         w_hi = pair_tiles("w_hi", ("buf_c", "buf_b"))
         round_pairs(w_hi, 0, w_raw[1], (36, 44))
         quantise_w(1, w_hi)

@@ -24,7 +24,9 @@ Q_HALF = Q // 2
 S_HALF = Q_HALF // PACK
 Y_HALF = I // 2
 RUN = 4
-Q_VECTOR_S = 32
+W_VECTOR = ((0, 0), (40, 44))
+Q_VECTOR = ((16, 48), (32, 64))
+WARM_M = 32
 Y_VECTOR_COLS = 320
 
 
@@ -50,39 +52,25 @@ def tile_attend_absorbscores_pl_kernel(tc, query, wuk, lat_words, lat_scales, of
         nc.sync.dma_start(lat_sc[32:96:4, :].bitcast(I32), lat_scales[0].bitcast(I32))
         key_sc = sb.tile([P, I], U8, name="key_sc", align_bytes=64)
         nc.vector.memset(key_sc[:].bitcast(I32), 0)
-        q_raw = [load_half("q_raw", q_rows, 0)]
         w_raw.append(load_half("w_raw", w_rows, 1))
-        q_raw.append(load_half("q_raw", q_rows, 1))
+        q_raw = [load_half("q_raw", q_rows, h) for h in range(2)]
         lat_w = sb.tile([P, T], U16, name="lat_w", tag="lat_w", align_bytes=64)
         nc.sync.dma_start(lat_w[:].bitcast(I32), lat_words[0].bitcast(I32))
 
         w_codes = sb.tile([P, C], U32, name="w_codes", align_bytes=64)
         w_sc = sb.tile([P, C], U8, name="w_sc", align_bytes=64)
-        b_bf = sb.tile([P, PACK, P, PACK], BF16, name="b_bf", align_bytes=64)
         M_HALF = P // 2
 
-        def pair_tiles(name, tags):
-            return [sb.tile([P, 2, M_HALF, PACK], BF16, name="%s%d" % (name, u), tag=tags[u], align_bytes=64) for u in range(2)]
+        def round_pair(pair, first, raw, u, cut):
+            src = raw[:].rearrange("p j (m t) -> p m j t", t=PACK)[:, :, :, 2 * u : 2 * u + 2]
+            dst = pair[:, :, first : first + M_HALF, :].rearrange("p t m j -> p m j t")
+            if cut > 0:
+                nc.vector.tensor_copy(dst[:, :cut], src[:, :cut])
+            if cut < M_HALF:
+                nc.scalar.activation(dst[:, cut:], src[:, cut:], ACT.Copy)
 
-        def round_pairs(pairs, first, raw, shares):
-            src = raw[:].rearrange("p j (m t) -> p m j t", t=PACK)
-            for u in range(2):
-                dst = pairs[u][:, :, first : first + M_HALF, :].rearrange("p t m j -> p m j t")
-                cut = shares[u]
-                if cut > 0:
-                    nc.vector.tensor_copy(dst[:, :cut], src[:, :cut, :, 2 * u : 2 * u + 2])
-                if cut < M_HALF:
-                    nc.scalar.activation(dst[:, cut:], src[:, cut:, :, 2 * u : 2 * u + 2], ACT.Copy)
-
-        def quantise_w(h, pairs):
-            for t in range(PACK):
-                cols = slice(t * P + h * M_HALF, t * P + (h + 1) * M_HALF)
-                nc.vector.quantize_mx(
-                    w_codes[:, cols].bitcast(FP8X4), w_sc[:, cols], pairs[t // 2][:, t % 2].rearrange("p m j -> p (m j)")
-                )
-
-        def quantise_q(name, pair, tag):
-            codes = sb.tile([P, P], U32, name=name + "_codes", tag=tag, align_bytes=64)
+        def quantise_q(name, pair):
+            codes = sb.tile([P, P], U32, name=name + "_codes", align_bytes=64)
             scales = sb.tile([P, P], U8, name=name + "_sc", align_bytes=64)
             nc.vector.quantize_mx(codes[:].bitcast(FP8X4), scales[:], pair[:].rearrange("p r s j -> p (r s j)"))
             return codes, scales
@@ -102,8 +90,6 @@ def tile_attend_absorbscores_pl_kernel(tc, query, wuk, lat_words, lat_scales, of
             b_dst = b_bf[:, 2 * v : 2 * v + 2, S_HALF * h : S_HALF * (h + 1), :]
             nc.scalar.activation(b_dst, b_ps[:].rearrange("p t (r s) -> p r s t", r=2), ACT.Copy)
 
-        w_lo = pair_tiles("w_lo", ("buf_a", "buf_b"))
-        round_pairs(w_lo, 0, w_raw[0], (0, 0))
         listed_sc = sb.tile([P, I], U8, name="listed_sc", align_bytes=64)
         nc.vector.tensor_copy(listed_sc[:], lat_sc[:].indirect(offsets[:]))
         for quad in range(QUADS):
@@ -112,32 +98,40 @@ def tile_attend_absorbscores_pl_kernel(tc, query, wuk, lat_words, lat_scales, of
                 listed_sc[32 + 16 * quad : 48 + 16 * quad : 4, :].bitcast(I32),
             )
 
-        quantise_w(0, w_lo)
-        q_lo = pair_tiles("q_lo", ("buf_c", "buf_d"))
-        round_pairs(q_lo, 0, q_raw[0], (0, 16))
-        first = quantise_q("q00", q_lo[0], "q00_codes")
-        warm_ps = ps.tile([32, P], F32, name="warm_ps", tag="a_ps3")
-        for warm in range(6):
+        w_pairs = [sb.tile([P, 2, P, PACK], BF16, name="w_pair%d" % u, align_bytes=64) for u in range(2)]
+        for h in range(2):
+            for u in range(2):
+                round_pair(w_pairs[u], h * M_HALF, w_raw[h], u, W_VECTOR[h][u])
+        for u in range(2):
+            cols = slice(2 * u * P, 2 * (u + 1) * P)
+            nc.vector.quantize_mx(w_codes[:, cols].bitcast(FP8X4), w_sc[:, cols], w_pairs[u][:].rearrange("p t m j -> p (t m j)"))
+
+        warm_ps = ps.tile([WARM_M, C], F32, name="warm_ps", tag="a_ps3")
+        for width in (P, P, P, P, C):
             nc.tensor.matmul_mx(
-                warm_ps[:],
-                lhsT=first[0][:, :32].bitcast(FP8X4),
-                lhsT_scale=first[1][:, :32],
-                rhs=first[0][:].bitcast(FP8X4),
-                rhs_scale=first[1][:],
+                warm_ps[:, :width],
+                lhsT=w_codes[:, :WARM_M].bitcast(FP8X4),
+                lhsT_scale=w_sc[:, :WARM_M],
+                rhs=w_codes[:, :width].bitcast(FP8X4),
+                rhs_scale=w_sc[:, :width],
                 start=True,
                 stop=True,
             )
-        w_hi = pair_tiles("w_hi", ("buf_c", "buf_b"))
-        round_pairs(w_hi, 0, w_raw[1], (36, 44))
-        quantise_w(1, w_hi)
-        bank(0, 0, first)
-        bank(0, 1, quantise_q("q01", q_lo[1], "buf_c"))
-        q_hi = pair_tiles("q_hi", ("buf_b", "buf_d"))
-        round_pairs(q_hi, 0, q_raw[1], (Q_VECTOR_S, M_HALF))
-        for v in range(2):
-            bank(1, v, quantise_q("q1%d" % v, q_hi[v], "q1%d_codes" % v))
 
-        key_w = sb.tile([P, I], U16, name="key_w", tag="q_raw1", align_bytes=64)
+        q_pairs = [
+            [sb.tile([P, 2, S_HALF, PACK], BF16, name="q_pair%d%d" % (h, v), align_bytes=64) for v in range(2)] for h in range(2)
+        ]
+        q_codes = []
+        for h in range(2):
+            for v in range(2):
+                round_pair(q_pairs[h][v], 0, q_raw[h], v, Q_VECTOR[h][v])
+            q_codes.append([quantise_q("q%d%d" % (h, v), q_pairs[h][v]) for v in range(2)])
+        b_bf = sb.tile([P, PACK, P, PACK], BF16, name="b_bf", align_bytes=64)
+        for h in range(2):
+            for v in range(2):
+                bank(h, v, q_codes[h][v])
+
+        key_w = sb.tile([P, I], U16, name="key_w", tag="q_pair11", align_bytes=64)
         nc.vector.tensor_copy(key_w[:], lat_w[:].indirect(offsets[:]))
 
         b_codes = sb.tile([P, Q], U32, name="b_codes", tag="lat_w", align_bytes=64)

@@ -25,8 +25,9 @@ S_HALF = Q_HALF // PACK
 Y_HALF = I // 2
 RUN = 4
 W_VECTOR = ((0, 0), (40, 44))
-Q_VECTOR = ((16, 48), (32, 64))
+Q_VECTOR = ((24, 40), (32, 64))
 WARM_M = 32
+WARM_PASSES = 5
 Y_VECTOR_COLS = 320
 
 
@@ -106,14 +107,14 @@ def tile_attend_absorbscores_pl_kernel(tc, query, wuk, lat_words, lat_scales, of
             cols = slice(2 * u * P, 2 * (u + 1) * P)
             nc.vector.quantize_mx(w_codes[:, cols].bitcast(FP8X4), w_sc[:, cols], w_pairs[u][:].rearrange("p t m j -> p (t m j)"))
 
-        warm_ps = ps.tile([WARM_M, C], F32, name="warm_ps", tag="a_ps3")
-        for width in (P, P, P, P, C):
+        warm_ps = ps.tile([WARM_M, P], F32, name="warm_ps", tag="a_ps3")
+        for warm in range(WARM_PASSES):
             nc.tensor.matmul_mx(
-                warm_ps[:, :width],
+                warm_ps[:],
                 lhsT=w_codes[:, :WARM_M].bitcast(FP8X4),
                 lhsT_scale=w_sc[:, :WARM_M],
-                rhs=w_codes[:, :width].bitcast(FP8X4),
-                rhs_scale=w_sc[:, :width],
+                rhs=w_codes[:, :P].bitcast(FP8X4),
+                rhs_scale=w_sc[:, :P],
                 start=True,
                 stop=True,
             )
@@ -131,10 +132,10 @@ def tile_attend_absorbscores_pl_kernel(tc, query, wuk, lat_words, lat_scales, of
             for v in range(2):
                 bank(h, v, q_codes[h][v])
 
-        key_w = sb.tile([P, I], U16, name="key_w", tag="q_pair11", align_bytes=64)
+        key_w = sb.tile([P, I], U16, name="key_w", tag="q_raw1", align_bytes=64)
         nc.vector.tensor_copy(key_w[:], lat_w[:].indirect(offsets[:]))
 
-        b_codes = sb.tile([P, Q], U32, name="b_codes", tag="lat_w", align_bytes=64)
+        b_codes = sb.tile([P, Q], U32, name="b_codes", align_bytes=64)
         b_sc = sb.tile([P, Q], U8, name="b_sc", align_bytes=64)
         neg_max = sb.tile([P, PACK], F32, name="neg_max")
         row_sum = sb.tile([P, PACK], F32, name="row_sum")

@@ -24,10 +24,10 @@ Q_HALF = Q // 2
 S_HALF = Q_HALF // PACK
 Y_HALF = I // 2
 RUN = 4
-W_VECTOR = ((0, 0), (40, 44))
-Q_VECTOR = ((24, 40), (32, 64))
+W_VECTOR = ((0, 48), (40, 40))
+Q_VECTOR = ((40, 0), (64, 64))
 WARM_M = 32
-WARM_PASSES = 5
+WARM_PASSES = 8
 Y_VECTOR_COLS = 320
 
 
@@ -47,14 +47,14 @@ def tile_attend_absorbscores_pl_kernel(tc, query, wuk, lat_words, lat_scales, of
 
         lat_sc = sb.tile([P, T], U8, name="lat_sc", align_bytes=64)
         nc.vector.memset(lat_sc[:].bitcast(I32), 0)
-        w_raw = [load_half("w_raw", w_rows, 0)]
+        q_raw = [load_half("q_raw", q_rows, 0)]
         offsets = sb.tile([P, I // 16], U16, name="offsets")
         nc.sync.dma_start(offsets[:], offs)
         nc.sync.dma_start(lat_sc[32:96:4, :].bitcast(I32), lat_scales[0].bitcast(I32))
         key_sc = sb.tile([P, I], U8, name="key_sc", align_bytes=64)
         nc.vector.memset(key_sc[:].bitcast(I32), 0)
-        w_raw.append(load_half("w_raw", w_rows, 1))
-        q_raw = [load_half("q_raw", q_rows, h) for h in range(2)]
+        w_raw = [load_half("w_raw", w_rows, h) for h in range(2)]
+        q_raw.append(load_half("q_raw", q_rows, 1))
         lat_w = sb.tile([P, T], U16, name="lat_w", tag="lat_w", align_bytes=64)
         nc.sync.dma_start(lat_w[:].bitcast(I32), lat_words[0].bitcast(I32))
 
@@ -91,6 +91,26 @@ def tile_attend_absorbscores_pl_kernel(tc, query, wuk, lat_words, lat_scales, of
             b_dst = b_bf[:, 2 * v : 2 * v + 2, S_HALF * h : S_HALF * (h + 1), :]
             nc.scalar.activation(b_dst, b_ps[:].rearrange("p t (r s) -> p r s t", r=2), ACT.Copy)
 
+        q_pairs = [
+            [sb.tile([P, 2, S_HALF, PACK], BF16, name="q_pair%d%d" % (h, v), align_bytes=64) for v in range(2)] for h in range(2)
+        ]
+        for v in range(2):
+            round_pair(q_pairs[0][v], 0, q_raw[0], v, Q_VECTOR[0][v])
+        q_codes = [[quantise_q("q00", q_pairs[0][0])]]
+
+        warm_codes, warm_sc = q_codes[0][0]
+        warm_ps = ps.tile([WARM_M, P], F32, name="warm_ps", tag="a_ps3")
+        for warm in range(WARM_PASSES):
+            nc.tensor.matmul_mx(
+                warm_ps[:],
+                lhsT=warm_codes[:, :WARM_M].bitcast(FP8X4),
+                lhsT_scale=warm_sc[:, :WARM_M],
+                rhs=warm_codes[:].bitcast(FP8X4),
+                rhs_scale=warm_sc[:],
+                start=True,
+                stop=True,
+            )
+
         listed_sc = sb.tile([P, I], U8, name="listed_sc", align_bytes=64)
         nc.vector.tensor_copy(listed_sc[:], lat_sc[:].indirect(offsets[:]))
         for quad in range(QUADS):
@@ -98,35 +118,20 @@ def tile_attend_absorbscores_pl_kernel(tc, query, wuk, lat_words, lat_scales, of
                 key_sc[32 * quad : 32 * quad + 4, :].bitcast(I32),
                 listed_sc[32 + 16 * quad : 48 + 16 * quad : 4, :].bitcast(I32),
             )
+        q_codes[0].append(quantise_q("q01", q_pairs[0][1]))
 
-        w_pairs = [sb.tile([P, 2, P, PACK], BF16, name="w_pair%d" % u, align_bytes=64) for u in range(2)]
         for h in range(2):
+            w_pairs = [sb.tile([P, 2, M_HALF, PACK], BF16, name="w_pair%d%d" % (h, u), align_bytes=64) for u in range(2)]
             for u in range(2):
-                round_pair(w_pairs[u], h * M_HALF, w_raw[h], u, W_VECTOR[h][u])
-        for u in range(2):
-            cols = slice(2 * u * P, 2 * (u + 1) * P)
-            nc.vector.quantize_mx(w_codes[:, cols].bitcast(FP8X4), w_sc[:, cols], w_pairs[u][:].rearrange("p t m j -> p (t m j)"))
+                round_pair(w_pairs[u], 0, w_raw[h], u, W_VECTOR[h][u])
+            for t in range(PACK):
+                cols = slice(t * P + h * M_HALF, t * P + (h + 1) * M_HALF)
+                src = w_pairs[t // 2][:, t % 2].rearrange("p m j -> p (m j)")
+                nc.vector.quantize_mx(w_codes[:, cols].bitcast(FP8X4), w_sc[:, cols], src)
 
-        warm_ps = ps.tile([WARM_M, P], F32, name="warm_ps", tag="a_ps3")
-        for warm in range(WARM_PASSES):
-            nc.tensor.matmul_mx(
-                warm_ps[:],
-                lhsT=w_codes[:, :WARM_M].bitcast(FP8X4),
-                lhsT_scale=w_sc[:, :WARM_M],
-                rhs=w_codes[:, :P].bitcast(FP8X4),
-                rhs_scale=w_sc[:, :P],
-                start=True,
-                stop=True,
-            )
-
-        q_pairs = [
-            [sb.tile([P, 2, S_HALF, PACK], BF16, name="q_pair%d%d" % (h, v), align_bytes=64) for v in range(2)] for h in range(2)
-        ]
-        q_codes = []
-        for h in range(2):
-            for v in range(2):
-                round_pair(q_pairs[h][v], 0, q_raw[h], v, Q_VECTOR[h][v])
-            q_codes.append([quantise_q("q%d%d" % (h, v), q_pairs[h][v]) for v in range(2)])
+        for v in range(2):
+            round_pair(q_pairs[1][v], 0, q_raw[1], v, Q_VECTOR[1][v])
+        q_codes.append([quantise_q("q1%d" % v, q_pairs[1][v]) for v in range(2)])
         b_bf = sb.tile([P, PACK, P, PACK], BF16, name="b_bf", align_bytes=64)
         for h in range(2):
             for v in range(2):

@@ -28,7 +28,7 @@ W_VECTOR = ((0, 48), (40, 40))
 Q_VECTOR = ((40, 0), (64, 64))
 WARM_M = 32
 WARM_PASSES = 8
-Y_VECTOR_COLS = 320
+Y_VECTOR_COLS = 352
 
 
 def tile_attend_absorbscores_pl_kernel(tc, query, wuk, lat_words, lat_scales, offs, out_0, out_1, out_2):

from contextlib import ExitStack

import concourse.mybir as mybir

D, C, T, I, Q = 512, 512, 2048, 512, 512
FLOPS = 2 * D * C * Q + 2 * C * Q * I

F32 = mybir.dt.float32
BF16 = mybir.dt.bfloat16
I32 = mybir.dt.int32
U32 = mybir.dt.uint32
U16 = mybir.dt.uint16
U8 = mybir.dt.uint8
FP8X4 = mybir.dt.float8_e4m3fn_x4
FP4X4 = mybir.dt.float4_e2m1fn_x4
ACT = mybir.ActivationFunctionType
ALU = mybir.AluOpType

P = 128
PACK = 4
QUADS = 4
OUT_SCALE = 512.0
Q_HALF = Q // 2
S_HALF = Q_HALF // PACK
Y_HALF = I // 2
RUN = 4
W_VECTOR = ((0, 48), (40, 40))
Q_VECTOR = ((40, 0), (64, 64))
WARM_M = 32
WARM_PASSES = 8
Y_VECTOR_COLS = 352


def tile_attend_absorbscores_pl_kernel(tc, query, wuk, lat_words, lat_scales, offs, out_0, out_1, out_2):
    nc = tc.nc
    with ExitStack() as ctx:
        sb = ctx.enter_context(tc.tile_pool(name="sb", bufs=1))
        ps = ctx.enter_context(tc.psum_pool(name="ps", bufs=1))

        w_rows = wuk.rearrange("(p j) c -> p j c", j=PACK)
        q_rows = query.rearrange("(p j) q -> p j q", j=PACK)

        def load_half(name, rows, h):
            half = sb.tile([P, PACK, Q_HALF], F32, name="%s%d" % (name, h), tag="%s%d" % (name, h), align_bytes=64)
            nc.sync.dma_start(half[:], rows[:, :, h * Q_HALF : (h + 1) * Q_HALF])
            return half

        lat_sc = sb.tile([P, T], U8, name="lat_sc", align_bytes=64)
        nc.vector.memset(lat_sc[:].bitcast(I32), 0)
        q_raw = [load_half("q_raw", q_rows, 0)]
        offsets = sb.tile([P, I // 16], U16, name="offsets")
        nc.sync.dma_start(offsets[:], offs)
        nc.sync.dma_start(lat_sc[32:96:4, :].bitcast(I32), lat_scales[0].bitcast(I32))
        key_sc = sb.tile([P, I], U8, name="key_sc", align_bytes=64)
        nc.vector.memset(key_sc[:].bitcast(I32), 0)
        w_raw = [load_half("w_raw", w_rows, h) for h in range(2)]
        q_raw.append(load_half("q_raw", q_rows, 1))
        lat_w = sb.tile([P, T], U16, name="lat_w", tag="lat_w", align_bytes=64)
        nc.sync.dma_start(lat_w[:].bitcast(I32), lat_words[0].bitcast(I32))

        w_codes = sb.tile([P, C], U32, name="w_codes", align_bytes=64)
        w_sc = sb.tile([P, C], U8, name="w_sc", align_bytes=64)
        M_HALF = P // 2

        def round_pair(pair, first, raw, u, cut):
            src = raw[:].rearrange("p j (m t) -> p m j t", t=PACK)[:, :, :, 2 * u : 2 * u + 2]
            dst = pair[:, :, first : first + M_HALF, :].rearrange("p t m j -> p m j t")
            if cut > 0:
                nc.vector.tensor_copy(dst[:, :cut], src[:, :cut])
            if cut < M_HALF:
                nc.scalar.activation(dst[:, cut:], src[:, cut:], ACT.Copy)

        def quantise_q(name, pair):
            codes = sb.tile([P, P], U32, name=name + "_codes", align_bytes=64)
            scales = sb.tile([P, P], U8, name=name + "_sc", align_bytes=64)
            nc.vector.quantize_mx(codes[:].bitcast(FP8X4), scales[:], pair[:].rearrange("p r s j -> p (r s j)"))
            return codes, scales

        def bank(h, v, operand):
            b_ps = ps.tile([P, PACK, P], F32, name="b_ps%d" % (2 * h + v))
            for t in range(PACK):
                nc.tensor.matmul_mx(
                    b_ps[:, t, :],
                    lhsT=w_codes[:, t * P : (t + 1) * P].bitcast(FP8X4),
                    lhsT_scale=w_sc[:, t * P : (t + 1) * P],
                    rhs=operand[0][:].bitcast(FP8X4),
                    rhs_scale=operand[1][:],
                    start=True,
                    stop=True,
                )
            b_dst = b_bf[:, 2 * v : 2 * v + 2, S_HALF * h : S_HALF * (h + 1), :]
            nc.scalar.activation(b_dst, b_ps[:].rearrange("p t (r s) -> p r s t", r=2), ACT.Copy)

        q_pairs = [
            [sb.tile([P, 2, S_HALF, PACK], BF16, name="q_pair%d%d" % (h, v), align_bytes=64) for v in range(2)] for h in range(2)
        ]
        for v in range(2):
            round_pair(q_pairs[0][v], 0, q_raw[0], v, Q_VECTOR[0][v])
        q_codes = [[quantise_q("q00", q_pairs[0][0])]]

        warm_codes, warm_sc = q_codes[0][0]
        warm_ps = ps.tile([WARM_M, P], F32, name="warm_ps", tag="a_ps3")
        for warm in range(WARM_PASSES):
            nc.tensor.matmul_mx(
                warm_ps[:],
                lhsT=warm_codes[:, :WARM_M].bitcast(FP8X4),
                lhsT_scale=warm_sc[:, :WARM_M],
                rhs=warm_codes[:].bitcast(FP8X4),
                rhs_scale=warm_sc[:],
                start=True,
                stop=True,
            )

        listed_sc = sb.tile([P, I], U8, name="listed_sc", align_bytes=64)
        nc.vector.tensor_copy(listed_sc[:], lat_sc[:].indirect(offsets[:]))
        for quad in range(QUADS):
            nc.sync.dma_start(
                key_sc[32 * quad : 32 * quad + 4, :].bitcast(I32),
                listed_sc[32 + 16 * quad : 48 + 16 * quad : 4, :].bitcast(I32),
            )
        q_codes[0].append(quantise_q("q01", q_pairs[0][1]))

        for h in range(2):
            w_pairs = [sb.tile([P, 2, M_HALF, PACK], BF16, name="w_pair%d%d" % (h, u), align_bytes=64) for u in range(2)]
            for u in range(2):
                round_pair(w_pairs[u], 0, w_raw[h], u, W_VECTOR[h][u])
            for t in range(PACK):
                cols = slice(t * P + h * M_HALF, t * P + (h + 1) * M_HALF)
                src = w_pairs[t // 2][:, t % 2].rearrange("p m j -> p (m j)")
                nc.vector.quantize_mx(w_codes[:, cols].bitcast(FP8X4), w_sc[:, cols], src)

        for v in range(2):
            round_pair(q_pairs[1][v], 0, q_raw[1], v, Q_VECTOR[1][v])
        q_codes.append([quantise_q("q1%d" % v, q_pairs[1][v]) for v in range(2)])
        b_bf = sb.tile([P, PACK, P, PACK], BF16, name="b_bf", align_bytes=64)
        for h in range(2):
            for v in range(2):
                bank(h, v, q_codes[h][v])

        key_w = sb.tile([P, I], U16, name="key_w", tag="q_raw1", align_bytes=64)
        nc.vector.tensor_copy(key_w[:], lat_w[:].indirect(offsets[:]))

        b_codes = sb.tile([P, Q], U32, name="b_codes", align_bytes=64)
        b_sc = sb.tile([P, Q], U8, name="b_sc", align_bytes=64)
        neg_max = sb.tile([P, PACK], F32, name="neg_max")
        row_sum = sb.tile([P, PACK], F32, name="row_sum")
        inv_sum = sb.tile([P, PACK], F32, name="inv_sum")
        prob = sb.tile([P, PACK, I], F32, name="prob")
        y = sb.tile([P, PACK, I], F32, name="y")
        y_rows = out_0.rearrange("(p r) i -> p r i", r=PACK)

        a_ps = []
        for first, last in ((0, 1), (1, 2), (2, PACK)):
            made = slice(first * P, last * P)
            nc.vector.quantize_mx(
                b_codes[:, made].bitcast(FP8X4), b_sc[:, made], b_bf[:, first:last].rearrange("p r s t -> p (r s t)")
            )
            for r in range(first, last):
                tile_cols = slice(r * P, (r + 1) * P)
                scores = ps.tile([P, I], F32, name="a_ps%d" % r, tag="a_ps%d" % r)
                nc.tensor.matmul_mx(
                    scores[:],
                    lhsT=b_codes[:, tile_cols].bitcast(FP8X4),
                    lhsT_scale=b_sc[:, tile_cols],
                    rhs=key_w[:].bitcast(FP4X4),
                    rhs_scale=key_sc[:],
                    start=True,
                    stop=True,
                )
                a_ps.append(scores)

        def exponentiate(r):
            nc.vector.tensor_reduce(neg_max[:, r : r + 1], a_ps[r][:], mybir.AxisListType.X, ALU.max, negate=True)
            nc.scalar.activation(
                prob[:, r, :], a_ps[r][:], ACT.Exp, bias=neg_max[:, r : r + 1], scale=1.0, accum_out=row_sum[:, r : r + 1]
            )

        def invert(r):
            nc.vector.reciprocal(inv_sum[:, r : r + 1], row_sum[:, r : r + 1])

        def normalise(r, slots):
            nc.vector.tensor_scalar(y[:, r, slots], prob[:, r, slots], inv_sum[:, r : r + 1], OUT_SCALE, ALU.mult, ALU.mult)

        def store(r):
            nc.sync.dma_start(y_rows[:, r, :], y[:, r, :])

        low, high, whole = slice(0, Y_HALF), slice(Y_HALF, I), slice(0, I)
        for r in range(PACK - 1):
            exponentiate(r)
        invert(0)
        exponentiate(3)
        normalise(0, whole)
        store(0)
        invert(1)
        invert(2)
        factor = sb.tile([P, 1], F32, name="factor")
        nc.vector.tensor_scalar(factor[:], inv_sum[:, 1:2], OUT_SCALE, None, ALU.mult)
        nc.scalar.activation(y[:, 1, :], prob[:, 1, :], ACT.Copy, scale=factor[:])
        normalise(2, low)
        invert(3)
        normalise(2, high)
        store(2)
        store(1)
        normalise(3, low)
        normalise(3, high)
        store(3)

        y_bf = sb.tile([P, I, PACK], BF16, name="y_bf", align_bytes=64)
        y_dst = y_bf[:].rearrange("p (g e) r -> p g r e", e=RUN)
        y_src = y[:].rearrange("p r (g e) -> p g r e", e=RUN)
        g_half = Y_HALF // RUN
        g_cut = Y_VECTOR_COLS // RUN
        nc.vector.tensor_copy(y_dst[:, :g_half], y_src[:, :g_half])
        nc.scalar.activation(y_dst[:, g_cut:], y_src[:, g_cut:], ACT.Copy)
        nc.vector.tensor_copy(y_dst[:, g_half:g_cut], y_src[:, g_half:g_cut])
        y_codes = sb.tile([P, I], U32, name="y_codes", align_bytes=64)
        y_sc = sb.tile([P, I], U8, name="y_sc", align_bytes=64)
        code_rows = out_1[0].rearrange("p i r -> p (i r)").bitcast(I32)
        for first in range(0, I, Y_HALF):
            slots = slice(first, first + Y_HALF)
            nc.vector.quantize_mx(
                y_codes[:, slots].bitcast(FP8X4), y_sc[:, slots], y_bf[:, slots, :].rearrange("p i r -> p (i r)")
            )
            nc.sync.dma_start(code_rows[:, slots], y_codes[:, slots].bitcast(I32))
        for quad in range(QUADS):
            queue = nc.scalar if quad == 0 else nc.sync
            queue.dma_start(
                out_2[0, 4 * quad : 4 * quad + 4, :].bitcast(I32),
                y_sc[32 * quad : 32 * quad + 4, :].bitcast(I32),
            )
